import numpy as np
CORES = [16,23,24,31,64,71]
N = 6
T, CAP, KR = 64, 32, 16
def entries(a): return a.T.reshape(-1)
def pack(v, P): return np.ascontiguousarray(np.asarray(v, np.int32).reshape(-1, P).T)
def lists(rng, how):
    D = np.stack([rng.permutation(np.repeat(np.arange(N), CAP))[:T] for r in range(N)])
    if how == "full": D = np.stack([(lambda q: rng.permutation(np.concatenate([np.repeat(q[:T // CAP], CAP), np.repeat(q[T // CAP:T // CAP + 1], T % CAP)])))(rng.permutation(N)) for r in range(N)])
    if how == "sorted": D = np.sort(D, axis=1)
    if how == "none": z = int(rng.integers(N)); D = np.stack([rng.permutation(np.repeat(np.delete(np.arange(N), z), CAP))[:T] for r in range(N)]) if CAP * (N - 1) >= T else D
    K_ = KR * D + (np.where(rng.random((N, T)) < 0.5, 0, KR - 1) if how == "edge" else rng.integers(0, KR, (N, T)))
    return {"key": np.stack([pack(K_[r], 16) for r in range(N)])}
def setup_inputs(rng):
    return dict({"x": rng.standard_normal((N, 128, T), dtype=np.float32)}, **lists(rng, "uniform"))
def setup_inputs_edge(rng):
    d = setup_inputs(rng); d.update(lists(rng, "edge"))
    for k in ("x",): d[k] = (d[k].astype(np.float32) * 1048576.0).astype(d[k].dtype)
    return d
def setup_inputs_full(rng):
    d = setup_inputs(rng); d.update(lists(rng, "full"))
    for k in ("x",): d[k] = (d[k].astype(np.float32) * (1 / 1024.0)).astype(d[k].dtype)
    return d
def setup_inputs_none(rng):
    d = setup_inputs(rng); d.update(lists(rng, "none"))
    return d
def setup_inputs_sorted(rng):
    d = setup_inputs(rng); d.update(lists(rng, "sorted"))
    return d
def check_inputs(x):
    bad = []
    if x["key"].min() < 0 or x["key"].max() >= N * KR: bad.append("key out of range")
    if max(int(np.bincount(entries(a) // KR, minlength=N).max()) for a in x["key"]) > CAP: bad.append("more than CAP columns of a rank go to one rank")
    return bad
def reference(x, key):
    y = np.zeros((N, 128, N * CAP), x.dtype)
    for r in range(N):
        D = entries(key[r]) // KR
        for d in range(N):
            got = x[r][:, D == d]; y[d][:, CAP * r:CAP * r + got.shape[1]] = got
    return {"y": y}

@@ -1,0 +1,233 @@
+from concourse.bass import DstId, RemoteDMATransfer
+from concourse.mybir import AluOpType as Op
+
+N = 6
+CAP = 32
+W = N * CAP
+
+SCRATCH = {
+    "xs": ("sbuf", [128, 64], "float32"),
+    "packed": ("sbuf", [128, W], "float32"),
+    "land": ("sbuf", [128, W], "float32"),
+    "kw": ("sbuf", [128, 4], "int32"),
+    "dw": ("sbuf", [128, 4], "int32"),
+    "ui": ("sbuf", [128, 2], "int32"),
+    "t1": ("sbuf", [128, 2], "int32"),
+    "t2": ("sbuf", [128, 2], "int32"),
+    "t3": ("sbuf", [128, 2], "int32"),
+    "offc": ("sbuf", [128, 2], "uint16"),
+    "patd": ("sbuf", [128, 32], "float32"),
+    "pat": ("sbuf", [128, 32], "float32"),
+    "rst": ("sbuf", [128, 32], "float32"),
+    "vv": ("sbuf", [128, 128], "float32"),
+    "la": ("sbuf", [128, 128], "float32"),
+    "lb": ("sbuf", [128, 128], "float32"),
+    "lh": ("sbuf", [128, 128], "bfloat16"),
+    "crow": ("sbuf", [128, 32], "bfloat16"),
+    "rh": ("sbuf", [128, 32], "bfloat16"),
+    "ps": ("psum", [128, 32], "float32"),
+    "seg": ("sbuf", [128, 32], "float32"),
+    "off": ("sbuf", [128, 4], "uint16"),
+    "rly": ("dram", [N, 128, CAP], "float32"),
+    "late": ("dram", [N, 128, CAP], "float32"),
+}
+SEMAPHORES = ["kl", "xl", "gu", "gd", "gp", "gv", "gcst", "vs", "lhr", "rhr", "mm", "scat", "own",
+              "dirs", "rin", "sent", "stored"] + ["late%d" % s for s in range(N)]
+
+
+def _bits(m):
+    return [e for e in range(m.bit_length()) if (m >> e) & 1]
+
+
+def _alloc(topo, src, items):
+    taken = set()
+    masks = [0] * len(items)
+    order = sorted(range(len(items)), key=lambda i: len(_bits(topo.mask(src, items[i][0]))))
+    for i in order:
+        to, n = items[i]
+        free = [e for e in _bits(topo.mask(src, to)) if e not in taken]
+        pick = free[-n:] if topo.chip(src) == topo.chip(to) else free[:n]
+        for e in pick:
+            taken.add(e)
+            masks[i] |= 1 << e
+    return masks
+
+
+def _plan(cores, topo):
+    sends = {c: [] for c in cores}
+    passes = {c: [] for c in cores}
+    for s, cs in enumerate(cores):
+        direct, relayed = [], []
+        for d, cd in enumerate(cores):
+            if d == s:
+                continue
+            if topo.may_write(cs, cd):
+                direct.append((d, cd))
+            else:
+                via = [c for c in cores if c != cs and topo.chip(c) == topo.chip(cs) and topo.may_write(c, cd)][0]
+                relayed.append((d, via))
+        total = max(len(_bits(topo.mask(cs, c))) for c in cores if c != cs)
+        first = [("rly", s, d, via, 4) for d, via in relayed]
+        left = total - 4 * len(relayed)
+        second = []
+        if left >= 2 * len(direct):
+            spare = left - 2 * len(direct)
+            for d, cd in direct:
+                n = 2
+                if relayed and topo.chip(cd) == topo.chip(cs) and spare >= 2:
+                    n, spare = 4, spare - 2
+                first.append(("dir", s, d, cd, n))
+        else:
+            second = [("dir", s, d, cd, 4) for d, cd in direct]
+        for call in (first, second):
+            if call:
+                masks = _alloc(topo, cs, [(t[3], t[4]) for t in call])
+                sends[cs].append([t + (m,) for t, m in zip(call, masks)])
+        for d, via in relayed:
+            passes[via].append((s, d))
+    hops = {}
+    for c in cores:
+        if passes[c]:
+            room = min(len(_bits(topo.mask(c, cores[d]))) for _, d in passes[c])
+            n = room // len(passes[c])
+            call = [("late", s, d, cores[d], n) for s, d in passes[c]]
+            masks = _alloc(topo, c, [(t[3], t[4]) for t in call])
+            hops[c] = [t + (m,) for t, m in zip(call, masks)]
+    return sends, hops
+
+
+def rank_program(g, core, T, topo):
+    rank = T.rank_of(core)
+    if rank is None:
+        return
+    cores = list(T.cores)
+    sends, hops = _plan(cores, topo)
+    S = T.sem
+    V, PE, SY, SC = g.vector, g.tensor, g.sync, g.scalar
+
+    n_dir = n_rin = 0
+    late_in = {}
+    for c in cores:
+        for call in sends[c]:
+            for kind, s, d, to, n, m in call:
+                if to == core and kind == "dir":
+                    n_dir += n
+                if to == core and kind == "rly":
+                    n_rin += n
+        for kind, s, d, to, n, m in hops.get(c, []):
+            if to == core:
+                late_in[s] = n
+
+    SC.dma_start(T.kw[0:16, :], T.key[:, :]).then_inc(S.kl, 16)
+    SY.dma_start(T.kw[32:48, :], T.key[:, :]).then_inc(S.kl, 16)
+    SC.dma_start(T.kw[16:32, :], T.key[:, :]).then_inc(S.kl, 16)
+    SY.dma_start(T.kw[48:64, :], T.key[:, :]).then_inc(S.kl, 16)
+    SY.dma_start(T.xs[:, :], T.x[:, :]).then_inc(S.xl, 16)
+
+    g.iota(T.ui[:, :], [[32, 2]], -48, 1).then_inc(S.gu, 1)
+    g.iota(T.patd[:, :], [[0, 4], [1, 8]], 0, 0, allow_small_or_imprecise_dtypes=True).then_inc(S.gd, 1)
+    g.iota(T.vv[0:64, :], [[0, 8], [1, 16]], 48, -1, allow_small_or_imprecise_dtypes=True).then_inc(S.gv, 1)
+    g.wait_ge(S.gd, 1)
+    g.affine_select(T.pat[:, :], T.patd[:, :], [[16, 4], [0, 8]], Op.is_ge, -1.0, -48, 1).then_inc(S.gp, 1)
+    g.iota(T.crow[0:1, :], [[0, 4], [32, 8]], -256, 0, allow_small_or_imprecise_dtypes=True).then_inc(S.gcst, 1)
+
+    nv = [0]
+
+    def vdone(ins):
+        ins.then_inc(S.vs, 1)
+        nv[0] += 1
+
+    def vsync():
+        V.wait_ge(S.vs, nv[0])
+
+    vdone(V.memset(T.kw[64:128, :], 0))
+    vdone(V.memset(T.packed[:, :], 0.0))
+    V.wait_ge(S.gu, 1)
+    vdone(V.tensor_scalar(T.t1[:, :], T.ui[:, :], 3, 1, Op.arith_shift_right, Op.bitwise_and))
+    vdone(V.tensor_scalar(T.t2[:, :], T.ui[:, :], 4, None, Op.arith_shift_right))
+    vsync()
+    vdone(V.tensor_tensor(T.t3[:, :], T.t1[:, :], T.t2[:, :], Op.add))
+    vsync()
+    vdone(V.tensor_scalar(T.offc[:, :], T.t3[:, :], 0, 3, Op.max, Op.min))
+    V.wait_ge(S.gv, 1)
+    vdone(V.tensor_scalar(T.la[0:64, :], T.vv[0:64, :], 0.0, None, Op.is_ge))
+    vdone(V.tensor_scalar(T.lb[0:64, :], T.vv[0:64, :], 0.0, 255.0, Op.is_equal, Op.mult))
+    vsync()
+    V.tensor_tensor(T.lh[0:64, :], T.la[0:64, :], T.lb[0:64, :], Op.add).then_inc(S.lhr, 1)
+    V.wait_ge(S.gd, 1)
+    vdone(V.tensor_scalar(T.rst[:, :], T.patd[:, :], 1.0, None, Op.min))
+    V.wait_ge(S.gp, 1)
+    V.wait_ge(S.kl, 64)
+    vsync()
+    vdone(V.tensor_scalar(T.dw[:, :], T.kw[:, :], 4, None, Op.arith_shift_right))
+    vsync()
+    V.tensor_tensor(T.rh[:, :], T.dw[:, 0:4].indirect(T.offc[:, 0:2]), T.pat[:, :], Op.is_equal).then_inc(S.rhr, 1)
+    V.wait_ge(S.mm, 1)
+    vdone(V.tensor_tensor_scan(T.seg[:, :], T.rst[:, :], T.ps[:, :], 0.0, Op.mult, Op.max))
+    vsync()
+    vdone(V.tensor_copy(T.off[:, :], T.seg[:, 7:32:8]))
+    V.wait_ge(S.xl, 16)
+    vsync()
+    V.tensor_copy(T.packed[:, 0:W].indirect(T.off[:, 0:4]), T.xs[:, :]).then_inc(S.scat, 1)
+    V.wait_ge(S.scat, 1)
+    V.tensor_copy(T.land[:, CAP * rank:CAP * rank + CAP], T.packed[:, CAP * rank:CAP * rank + CAP]).then_inc(S.own, 1)
+
+    PE.wait_ge(S.lhr, 1)
+    PE.wait_ge(S.gcst, 1)
+    PE.matmul(T.ps[:, :], T.lh[0:1, :], T.crow[0:1, :], True, False)
+    PE.wait_ge(S.rhr, 1)
+    PE.matmul(T.ps[:, :], T.lh[0:64, :], T.rh[0:64, :], False, True).then_inc(S.mm, 1)
+
+    n_sent = 0
+
+    def fused(call):
+        trs = []
+        cnt = 0
+        for kind, s, d, to, n, m in call:
+            rid, pid, _ = topo.addr(to)
+            if kind == "dir":
+                src, dst, sem = T.packed[:, CAP * d:CAP * d + CAP], T.land[:, CAP * s:CAP * s + CAP], S.dirs
+            elif kind == "rly":
+                src, dst, sem = T.packed[:, CAP * d:CAP * d + CAP], T.rly[d], S.rin
+            else:
+                src, dst, sem = T.rly[d], T.late[s], S["late%d" % s]
+            trs.append(RemoteDMATransfer(dst_ids=[DstId(rid=rid, pnc=pid)], dma_engine_mask=m, remote_sem=sem,
+                                         src=src, dst=dst))
+            cnt += n
+        g.remote_dma_fused(trs, local_sem=S.sent)
+        return cnt
+
+    g.wait_ge(S.scat, 1)
+    for call in sends[core]:
+        n_sent += fused(call)
+    if core in hops:
+        g.wait_ge(S.rin, n_rin)
+        n_sent += fused(hops[core])
+
+    runs = []
+    for b in range(N):
+        if b in late_in:
+            continue
+        if runs and runs[-1][1] == b:
+            runs[-1][1] = b + 1
+        else:
+            runs.append([b, b + 1])
+    queues = [SY, SC]
+    n_st = 0
+    waited = set()
+    for i, (a, b) in enumerate(sorted(runs, key=lambda r: r[1] - r[0])):
+        q = queues[i % 2]
+        if i % 2 not in waited:
+            q.wait_ge(S.dirs, n_dir)
+            q.wait_ge(S.own, 1)
+            waited.add(i % 2)
+        q.dma_start(T.y[:, CAP * a:CAP * b], T.land[:, CAP * a:CAP * b]).then_inc(S.stored, 16)
+        n_st += 1
+    for i, s in enumerate(sorted(late_in)):
+        q = queues[i % 2]
+        q.wait_ge(S["late%d" % s], late_in[s])
+        q.dma_start(T.y[:, CAP * s:CAP * s + CAP], T.late[s]).then_inc(S.stored, 16)
+        n_st += 1
+
+    g.wait_ge(S.sent, n_sent)
+    g.wait_ge(S.stored, 16 * n_st)

@@ -7,10 +7,14 @@ W = N * CAP
 
 SCRATCH = {
     "xs": ("sbuf", [128, 64], "float32"),
+    "xn": ("sbuf", [128, 64], "float32"),
     "packed": ("sbuf", [128, W], "float32"),
+    "tmp": ("sbuf", [128, W], "float32"),
     "land": ("sbuf", [128, W], "float32"),
     "kw": ("sbuf", [128, 4], "int32"),
+    "kn": ("sbuf", [128, 4], "int32"),
     "dw": ("sbuf", [128, 4], "int32"),
+    "dn": ("sbuf", [128, 4], "int32"),
     "ui": ("sbuf", [128, 2], "int32"),
     "t1": ("sbuf", [128, 2], "int32"),
     "t2": ("sbuf", [128, 2], "int32"),
@@ -25,18 +29,29 @@ SCRATCH = {
     "lh": ("sbuf", [128, 128], "bfloat16"),
     "crow": ("sbuf", [128, 32], "bfloat16"),
     "rh": ("sbuf", [128, 32], "bfloat16"),
-    "ps": ("psum", [128, 32], "float32"),
+    "rn": ("sbuf", [128, 32], "bfloat16"),
+    "ps": ("psum", [128, 512], "float32"),
+    "pn": ("psum", [128, 512], "float32"),
     "seg": ("sbuf", [128, 32], "float32"),
+    "sn": ("sbuf", [128, 32], "float32"),
     "off": ("sbuf", [128, 4], "uint16"),
+    "offn": ("sbuf", [128, 4], "uint16"),
     "rly": ("dram", [N, 128, CAP], "float32"),
     "late": ("dram", [N, 128, CAP], "float32"),
 }
-SEMAPHORES = ["kl", "xl", "gu", "gd", "gp", "gv", "gcst", "vs", "lhr", "rhr", "mm", "scat", "own",
-              "dirs", "rin", "sent", "stored"] + ["late%d" % s for s in range(N)]
+SEMAPHORES = ["kl", "xl", "kz", "gu", "gd", "gp", "gv", "gcst", "vs", "lhr", "rhr", "mm", "rhn", "mmn", "scat", "scatn",
+              "own", "nbr", "kin", "xin", "dirs", "rin", "sent", "stored"] + ["late%d" % s for s in range(N)]
 
 
 def _bits(m):
     return [e for e in range(m.bit_length()) if (m >> e) & 1]
+
+
+def _pow2(n):
+    p = 1
+    while 2 * p <= n:
+        p *= 2
+    return p
 
 
 def _alloc(topo, src, items):
@@ -54,46 +69,39 @@ def _alloc(topo, src, items):
 
 
 def _plan(cores, topo):
-    sends = {c: [] for c in cores}
+    main, hops, kmask, xmask, nbr = {}, {}, {}, {}, {}
     passes = {c: [] for c in cores}
     for s, cs in enumerate(cores):
+        nbr[cs] = [c for c in cores if c != cs and topo.chip(c) == topo.chip(cs)][0]
         direct, relayed = [], []
         for d, cd in enumerate(cores):
-            if d == s:
+            if cd == cs or cd == nbr[cs]:
                 continue
             if topo.may_write(cs, cd):
                 direct.append((d, cd))
             else:
-                via = [c for c in cores if c != cs and topo.chip(c) == topo.chip(cs) and topo.may_write(c, cd)][0]
-                relayed.append((d, via))
-        total = max(len(_bits(topo.mask(cs, c))) for c in cores if c != cs)
-        first = [("rly", s, d, via, 4) for d, via in relayed]
-        left = total - 4 * len(relayed)
-        second = []
-        if left >= 2 * len(direct):
-            spare = left - 2 * len(direct)
-            for d, cd in direct:
-                n = 2
-                if relayed and topo.chip(cd) == topo.chip(cs) and spare >= 2:
-                    n, spare = 4, spare - 2
-                first.append(("dir", s, d, cd, n))
-        else:
-            second = [("dir", s, d, cd, 4) for d, cd in direct]
-        for call in (first, second):
-            if call:
-                masks = _alloc(topo, cs, [(t[3], t[4]) for t in call])
-                sends[cs].append([t + (m,) for t, m in zip(call, masks)])
-        for d, via in relayed:
-            passes[via].append((s, d))
-    hops = {}
+                relayed.append((d, nbr[cs]))
+                passes[nbr[cs]].append((s, d))
+        every = _bits(topo.mask(cs, nbr[cs]))
+        call = [("rly", s, d, via, 4) for d, via in relayed]
+        if direct:
+            room = min(min(len(_bits(topo.mask(cs, cd))) for _, cd in direct), len(every) - 4 * len(relayed))
+            call += [("dir", s, d, cd, _pow2(room // len(direct))) for d, cd in direct]
+        masks = _alloc(topo, cs, [(t[3], t[4]) for t in call])
+        main[cs] = [t + (m,) for t, m in zip(call, masks)]
+        used = 0
+        for m in masks:
+            used |= m
+        kmask[cs] = used
+        rest = [e for e in every if not (used >> e) & 1]
+        xmask[cs] = sum(1 << e for e in rest) if rest else used
     for c in cores:
         if passes[c]:
             room = min(len(_bits(topo.mask(c, cores[d]))) for _, d in passes[c])
-            n = room // len(passes[c])
-            call = [("late", s, d, cores[d], n) for s, d in passes[c]]
+            call = [("late", s, d, cores[d], _pow2(room // len(passes[c]))) for s, d in passes[c]]
             masks = _alloc(topo, c, [(t[3], t[4]) for t in call])
             hops[c] = [t + (m,) for t, m in zip(call, masks)]
-    return sends, hops
+    return main, hops, kmask, xmask, nbr
 
 
 def rank_program(g, core, T, topo):
@@ -101,22 +109,25 @@ def rank_program(g, core, T, topo):
     if rank is None:
         return
     cores = list(T.cores)
-    sends, hops = _plan(cores, topo)
+    main, hops, kmask, xmask, nbrs = _plan(cores, topo)
+    nb = nbrs[core]
+    nrank = T.rank_of(nb)
     S = T.sem
     V, PE, SY, SC = g.vector, g.tensor, g.sync, g.scalar
 
     n_dir = n_rin = 0
     late_in = {}
     for c in cores:
-        for call in sends[c]:
-            for kind, s, d, to, n, m in call:
-                if to == core and kind == "dir":
-                    n_dir += n
-                if to == core and kind == "rly":
-                    n_rin += n
+        for kind, s, d, to, n, m in main[c]:
+            if to == core and kind == "dir":
+                n_dir += n
+            if to == core and kind == "rly":
+                n_rin += n
         for kind, s, d, to, n, m in hops.get(c, []):
             if to == core:
                 late_in[s] = n
+    n_kin = len(_bits(kmask[nb]))
+    n_xin = len(_bits(xmask[nb]))
 
     SC.dma_start(T.kw[0:16, :], T.key[:, :]).then_inc(S.kl, 16)
     SY.dma_start(T.kw[32:48, :], T.key[:, :]).then_inc(S.kl, 16)
@@ -140,7 +151,16 @@ def rank_program(g, core, T, topo):
     def vsync():
         V.wait_ge(S.vs, nv[0])
 
-    vdone(V.memset(T.kw[64:128, :], 0))
+    def slots(kt, dt_, rt, pt, st, ot, sem_r, sem_m):
+        vdone(V.tensor_scalar(dt_[:, :], kt[:, :], 4, None, Op.arith_shift_right))
+        vsync()
+        V.tensor_tensor(rt[:, :], dt_[:, 0:4].indirect(T.offc[:, 0:2]), T.pat[:, :], Op.is_equal).then_inc(sem_r, 1)
+        V.wait_ge(sem_m, 1)
+        vdone(V.tensor_tensor_scan(st[:, :], T.rst[:, :], pt[:, 0:32], 0.0, Op.mult, Op.max))
+        vsync()
+        vdone(V.tensor_copy(ot[:, :], st[:, 7:32:8]))
+
+    V.memset(T.kw[64:128, :], 0).then_inc(S.kz, 1)
     vdone(V.memset(T.packed[:, :], 0.0))
     V.wait_ge(S.gu, 1)
     vdone(V.tensor_scalar(T.t1[:, :], T.ui[:, :], 3, 1, Op.arith_shift_right, Op.bitwise_and))
@@ -157,28 +177,33 @@ def rank_program(g, core, T, topo):
     V.wait_ge(S.gd, 1)
     vdone(V.tensor_scalar(T.rst[:, :], T.patd[:, :], 1.0, None, Op.min))
     V.wait_ge(S.gp, 1)
+    V.wait_ge(S.kz, 1)
     V.wait_ge(S.kl, 64)
     vsync()
-    vdone(V.tensor_scalar(T.dw[:, :], T.kw[:, :], 4, None, Op.arith_shift_right))
-    vsync()
-    V.tensor_tensor(T.rh[:, :], T.dw[:, 0:4].indirect(T.offc[:, 0:2]), T.pat[:, :], Op.is_equal).then_inc(S.rhr, 1)
-    V.wait_ge(S.mm, 1)
-    vdone(V.tensor_tensor_scan(T.seg[:, :], T.rst[:, :], T.ps[:, :], 0.0, Op.mult, Op.max))
-    vsync()
-    vdone(V.tensor_copy(T.off[:, :], T.seg[:, 7:32:8]))
+    slots(T.kw, T.dw, T.rh, T.ps, T.seg, T.off, S.rhr, S.mm)
     V.wait_ge(S.xl, 16)
     vsync()
     V.tensor_copy(T.packed[:, 0:W].indirect(T.off[:, 0:4]), T.xs[:, :]).then_inc(S.scat, 1)
     V.wait_ge(S.scat, 1)
-    V.tensor_copy(T.land[:, CAP * rank:CAP * rank + CAP], T.packed[:, CAP * rank:CAP * rank + CAP]).then_inc(S.own, 1)
+    me = slice(CAP * rank, CAP * rank + CAP)
+    V.tensor_copy(T.land[:, me], T.packed[:, me]).then_inc(S.own, 1)
+    vdone(V.memset(T.tmp[:, :], 0.0))
+    V.wait_ge(S.kin, n_kin)
+    slots(T.kn, T.dn, T.rn, T.pn, T.sn, T.offn, S.rhn, S.mmn)
+    V.wait_ge(S.xin, n_xin)
+    vsync()
+    V.tensor_copy(T.tmp[:, 0:W].indirect(T.offn[:, 0:4]), T.xn[:, :]).then_inc(S.scatn, 1)
+    V.wait_ge(S.scatn, 1)
+    V.tensor_copy(T.land[:, CAP * nrank:CAP * nrank + CAP], T.tmp[:, me]).then_inc(S.nbr, 1)
 
     PE.wait_ge(S.lhr, 1)
     PE.wait_ge(S.gcst, 1)
-    PE.matmul(T.ps[:, :], T.lh[0:1, :], T.crow[0:1, :], True, False)
+    PE.matmul(T.ps[:, 0:32], T.lh[0:1, :], T.crow[0:1, :], True, False)
     PE.wait_ge(S.rhr, 1)
-    PE.matmul(T.ps[:, :], T.lh[0:64, :], T.rh[0:64, :], False, True).then_inc(S.mm, 1)
-
-    n_sent = 0
+    PE.matmul(T.ps[:, 0:32], T.lh[0:64, :], T.rh[0:64, :], False, True).then_inc(S.mm, 1)
+    PE.matmul(T.pn[:, 0:32], T.lh[0:1, :], T.crow[0:1, :], True, False)
+    PE.wait_ge(S.rhn, 1)
+    PE.matmul(T.pn[:, 0:32], T.lh[0:64, :], T.rn[0:64, :], False, True).then_inc(S.mmn, 1)
 
     def fused(call):
         trs = []
@@ -197,9 +222,15 @@ def rank_program(g, core, T, topo):
         g.remote_dma_fused(trs, local_sem=S.sent)
         return cnt
 
+    nrid, npid, _ = topo.addr(nb)
+    g.wait_ge(S.kz, 1)
+    g.wait_ge(S.kl, 64)
+    g.remote_dma(T.kn[:, :], T.kw[:, :], S.kin, S.sent, npid, nrid, kmask[core])
+    n_sent = len(_bits(kmask[core]))
     g.wait_ge(S.scat, 1)
-    for call in sends[core]:
-        n_sent += fused(call)
+    n_sent += fused(main[core])
+    g.remote_dma(T.xn[:, :], T.xs[:, :], S.xin, S.sent, npid, nrid, xmask[core])
+    n_sent += len(_bits(xmask[core]))
     if core in hops:
         g.wait_ge(S.rin, n_rin)
         n_sent += fused(hops[core])
@@ -212,21 +243,16 @@ def rank_program(g, core, T, topo):
             runs[-1][1] = b + 1
         else:
             runs.append([b, b + 1])
-    queues = [SY, SC]
     n_st = 0
-    waited = set()
-    for i, (a, b) in enumerate(sorted(runs, key=lambda r: r[1] - r[0])):
-        q = queues[i % 2]
-        if i % 2 not in waited:
-            q.wait_ge(S.dirs, n_dir)
-            q.wait_ge(S.own, 1)
-            waited.add(i % 2)
-        q.dma_start(T.y[:, CAP * a:CAP * b], T.land[:, CAP * a:CAP * b]).then_inc(S.stored, 16)
+    SC.wait_ge(S.dirs, n_dir)
+    SC.wait_ge(S.own, 1)
+    SC.wait_ge(S.nbr, 1)
+    for a, b in runs:
+        SC.dma_start(T.y[:, CAP * a:CAP * b], T.land[:, CAP * a:CAP * b]).then_inc(S.stored, 16)
         n_st += 1
-    for i, s in enumerate(sorted(late_in)):
-        q = queues[i % 2]
-        q.wait_ge(S["late%d" % s], late_in[s])
-        q.dma_start(T.y[:, CAP * s:CAP * s + CAP], T.late[s]).then_inc(S.stored, 16)
+    for s in sorted(late_in):
+        SY.wait_ge(S["late%d" % s], late_in[s])
+        SY.dma_start(T.y[:, CAP * s:CAP * s + CAP], T.late[s]).then_inc(S.stored, 16)
         n_st += 1
 
     g.wait_ge(S.sent, n_sent)

@@ -1,9 +1,11 @@
 from concourse.bass import DstId, RemoteDMATransfer
 from concourse.mybir import AluOpType as Op
+from concourse.mybir import ActivationFunctionType as Act
 
 N = 6
 CAP = 32
 W = N * CAP
+DW = 12
 
 SCRATCH = {
     "xs": ("sbuf", [128, 64], "float32"),
@@ -13,23 +15,23 @@ SCRATCH = {
     "land": ("sbuf", [128, W], "float32"),
     "kw": ("sbuf", [128, 4], "int32"),
     "kn": ("sbuf", [128, 4], "int32"),
-    "dw": ("sbuf", [128, 4], "int32"),
-    "dn": ("sbuf", [128, 4], "int32"),
+    "dw": ("sbuf", [128, DW], "int32"),
+    "dn": ("sbuf", [128, DW], "int32"),
     "ui": ("sbuf", [128, 2], "int32"),
     "t1": ("sbuf", [128, 2], "int32"),
     "t2": ("sbuf", [128, 2], "int32"),
     "t3": ("sbuf", [128, 2], "int32"),
     "offc": ("sbuf", [128, 2], "uint16"),
     "patd": ("sbuf", [128, 32], "float32"),
-    "pat": ("sbuf", [128, 32], "float32"),
     "rst": ("sbuf", [128, 32], "float32"),
-    "vv": ("sbuf", [128, 128], "float32"),
-    "la": ("sbuf", [128, 128], "float32"),
-    "lb": ("sbuf", [128, 128], "float32"),
+    "vv": ("sbuf", [128, 128], "bfloat16"),
+    "la": ("sbuf", [128, 128], "bfloat16"),
+    "lb": ("sbuf", [128, 128], "bfloat16"),
     "lh": ("sbuf", [128, 128], "bfloat16"),
+    "on": ("sbuf", [128, 128], "bfloat16"),
     "crow": ("sbuf", [128, 32], "bfloat16"),
-    "rh": ("sbuf", [128, 32], "bfloat16"),
-    "rn": ("sbuf", [128, 32], "bfloat16"),
+    "rh": ("sbuf", [128, 48], "bfloat16"),
+    "rn": ("sbuf", [128, 48], "bfloat16"),
     "ps": ("psum", [128, 512], "float32"),
     "pn": ("psum", [128, 512], "float32"),
     "seg": ("sbuf", [128, 32], "float32"),
@@ -39,69 +41,69 @@ SCRATCH = {
     "rly": ("dram", [N, 128, CAP], "float32"),
     "late": ("dram", [N, 128, CAP], "float32"),
 }
-SEMAPHORES = ["kl", "xl", "kz", "gu", "gd", "gp", "gv", "gcst", "vs", "lhr", "rhr", "mm", "rhn", "mmn", "scat", "scatn",
-              "own", "nbr", "kin", "xin", "dirs", "rin", "sent", "stored"] + ["late%d" % s for s in range(N)]
+SEMAPHORES = (["kl", "xl", "kz", "dz", "dwr", "dnr", "gu", "gd", "gv", "gcst", "cz", "arh", "apk", "arst", "arn", "atmp",
+               "vs", "lhr", "rhr", "mm", "rhn", "mmn", "scat", "scatn", "kin", "xin", "sent", "stored", "rin0", "rin1"]
+              + ["late%d" % s for s in range(N)] + ["in%d" % s for s in range(N)])
 
 
 def _bits(m):
     return [e for e in range(m.bit_length()) if (m >> e) & 1]
 
 
-def _pow2(n):
-    p = 1
-    while 2 * p <= n:
-        p *= 2
-    return p
+def _mask(engs):
+    return sum(1 << e for e in engs)
 
 
-def _alloc(topo, src, items):
-    taken = set()
-    masks = [0] * len(items)
-    order = sorted(range(len(items)), key=lambda i: len(_bits(topo.mask(src, items[i][0]))))
-    for i in order:
-        to, n = items[i]
-        free = [e for e in _bits(topo.mask(src, to)) if e not in taken]
-        pick = free[-n:] if topo.chip(src) == topo.chip(to) else free[:n]
-        for e in pick:
-            taken.add(e)
-            masks[i] |= 1 << e
-    return masks
+def _split(engs, k):
+    n = 1
+    while 2 * n * k <= len(engs):
+        n *= 2
+    return [engs[i * n:(i + 1) * n] for i in range(k)]
 
 
 def _plan(cores, topo):
-    main, hops, kmask, xmask, nbr = {}, {}, {}, {}, {}
-    passes = {c: [] for c in cores}
-    for s, cs in enumerate(cores):
-        nbr[cs] = [c for c in cores if c != cs and topo.chip(c) == topo.chip(cs)][0]
-        direct, relayed = [], []
-        for d, cd in enumerate(cores):
-            if cd == cs or cd == nbr[cs]:
-                continue
-            if topo.may_write(cs, cd):
-                direct.append((d, cd))
-            else:
-                relayed.append((d, nbr[cs]))
-                passes[nbr[cs]].append((s, d))
-        every = _bits(topo.mask(cs, nbr[cs]))
-        call = [("rly", s, d, via, 4) for d, via in relayed]
-        if direct:
-            room = min(min(len(_bits(topo.mask(cs, cd))) for _, cd in direct), len(every) - 4 * len(relayed))
-            call += [("dir", s, d, cd, _pow2(room // len(direct))) for d, cd in direct]
-        masks = _alloc(topo, cs, [(t[3], t[4]) for t in call])
-        main[cs] = [t + (m,) for t, m in zip(call, masks)]
-        used = 0
-        for m in masks:
-            used |= m
-        kmask[cs] = used
-        rest = [e for e in every if not (used >> e) & 1]
-        xmask[cs] = sum(1 << e for e in rest) if rest else used
-    for c in cores:
-        if passes[c]:
-            room = min(len(_bits(topo.mask(c, cores[d]))) for _, d in passes[c])
-            call = [("late", s, d, cores[d], _pow2(room // len(passes[c]))) for s, d in passes[c]]
-            masks = _alloc(topo, c, [(t[3], t[4]) for t in call])
-            hops[c] = [t + (m,) for t, m in zip(call, masks)]
-    return main, hops, kmask, xmask, nbr
+    n = len(cores)
+    chip = [topo.chip(c) for c in cores]
+    on_chip = {}
+    for r in range(n):
+        on_chip.setdefault(chip[r], []).append(r)
+    nbr = [[q for q in on_chip[chip[r]] if q != r][0] for r in range(n)]
+
+    def one_link(a, b):
+        return 1 if (topo.mates(a, b) or topo.same_plane(a, b)) else 0
+
+    def reach(r, ch):
+        return all(topo.may_write(cores[r], cores[d]) for d in on_chip[ch])
+
+    far = [sorted([ch for ch in on_chip if ch != chip[r]], key=lambda ch: (one_link(chip[r], ch), ch)) for r in range(n)]
+    passes = [[] for _ in range(n)]
+    for r in range(n):
+        for ch in far[r]:
+            if not reach(r, ch):
+                passes[nbr[r]].append((r, ch))
+
+    calls = [[] for _ in range(n)]
+    kmask, xmask = [0] * n, [0] * n
+    for r in range(n):
+        every = _bits(topo.mask(cores[r], cores[nbr[r]]))
+        out = [e for e in every if all((topo.mask(cores[r], cores[d]) >> e) & 1 for d in range(n) if chip[d] != chip[r])]
+        mine = [ch for ch in far[r] if reach(r, ch)]
+        relayed = [ch for ch in far[r] if not reach(r, ch)]
+        for ch in relayed:
+            parts = _split(every, len(on_chip[ch]))
+            sem = "rin%d" % passes[nbr[r]].index((r, ch))
+            calls[r].append((None, [("rly", r, d, nbr[r], parts[i], sem) for i, d in enumerate(on_chip[ch])]))
+        db = [d for ch in mine for d in on_chip[ch]]
+        if db:
+            parts = _split(out, len(db))
+            calls[r].append((None, [("dir", r, d, d, parts[i], "in%d" % r) for i, d in enumerate(db)]))
+        used = every if relayed else out
+        free = [e for e in every if e not in used]
+        kmask[r], xmask[r] = _mask(used), _mask(free if free else used)
+        for i, (s, ch) in enumerate(passes[r]):
+            parts = _split(out, len(on_chip[ch]))
+            calls[r].append(("rin%d" % i, [("late", s, d, d, parts[j], "late%d" % s) for j, d in enumerate(on_chip[ch])]))
+    return calls, kmask, xmask, nbr
 
 
 def rank_program(g, core, T, topo):
@@ -109,38 +111,43 @@ def rank_program(g, core, T, topo):
     if rank is None:
         return
     cores = list(T.cores)
-    main, hops, kmask, xmask, nbrs = _plan(cores, topo)
-    nb = nbrs[core]
-    nrank = T.rank_of(nb)
+    calls, kmask, xmask, nbrs = _plan(cores, topo)
+    nrank = nbrs[rank]
+    nb = cores[nrank]
     S = T.sem
     V, PE, SY, SC = g.vector, g.tensor, g.sync, g.scalar
 
-    n_dir = n_rin = 0
-    late_in = {}
-    for c in cores:
-        for kind, s, d, to, n, m in main[c]:
-            if to == core and kind == "dir":
-                n_dir += n
-            if to == core and kind == "rly":
-                n_rin += n
-        for kind, s, d, to, n, m in hops.get(c, []):
-            if to == core:
-                late_in[s] = n
-    n_kin = len(_bits(kmask[nb]))
-    n_xin = len(_bits(xmask[nb]))
+    arrive = {}
+    for r in range(N):
+        for _, trs in calls[r]:
+            for kind, s, d, to, engs, sem in trs:
+                if to == rank:
+                    arrive[sem] = arrive.get(sem, 0) + len(engs)
+    late_in = [s for s in range(N) if "late%d" % s in arrive]
+    n_kin = len(_bits(kmask[nrank]))
+    n_xin = len(_bits(xmask[nrank]))
+
+    def blk(b):
+        return slice(CAP * b, CAP * b + CAP)
 
     SC.dma_start(T.kw[0:16, :], T.key[:, :]).then_inc(S.kl, 16)
-    SY.dma_start(T.kw[32:48, :], T.key[:, :]).then_inc(S.kl, 16)
-    SC.dma_start(T.kw[16:32, :], T.key[:, :]).then_inc(S.kl, 16)
-    SY.dma_start(T.kw[48:64, :], T.key[:, :]).then_inc(S.kl, 16)
+    SY.dma_start(T.kw[16:32, :], T.key[:, :]).then_inc(S.kl, 16)
     SY.dma_start(T.xs[:, :], T.x[:, :]).then_inc(S.xl, 16)
 
-    g.iota(T.ui[:, :], [[32, 2]], -48, 1).then_inc(S.gu, 1)
+    g.iota(T.ui[:, :], [[32, 2]], 0, 1).then_inc(S.gu, 1)
+    g.iota(T.vv[0:32, :], [[0, 8], [1, 16]], 16, -1, allow_small_or_imprecise_dtypes=True).then_inc(S.gv, 1)
     g.iota(T.patd[:, :], [[0, 4], [1, 8]], 0, 0, allow_small_or_imprecise_dtypes=True).then_inc(S.gd, 1)
-    g.iota(T.vv[0:64, :], [[0, 8], [1, 16]], 48, -1, allow_small_or_imprecise_dtypes=True).then_inc(S.gv, 1)
-    g.wait_ge(S.gd, 1)
-    g.affine_select(T.pat[:, :], T.patd[:, :], [[16, 4], [0, 8]], Op.is_ge, -1.0, -48, 1).then_inc(S.gp, 1)
-    g.iota(T.crow[0:1, :], [[0, 4], [32, 8]], -256, 0, allow_small_or_imprecise_dtypes=True).then_inc(S.gcst, 1)
+
+    SC.wait_ge(S.cz, 1)
+    SC.activation(T.rh[:, 0:16], T.on[:, 0:16], Act.Copy, scale=0.0).then_inc(S.arh, 1)
+    SC.activation(T.packed[:, 0:128], T.on[:, 0:128], Act.Copy, scale=0.0).then_inc(S.apk, 1)
+    SC.activation(T.packed[:, 128:W], T.on[:, 0:W - 128], Act.Copy, scale=0.0).then_inc(S.apk, 1)
+    SC.wait_ge(S.gd, 1)
+    SC.activation(T.crow[0:1, :], T.patd[0:1, :], Act.Identity, bias=-256.0, scale=32.0).then_inc(S.gcst, 1)
+    SC.activation(T.rst[:, :], T.patd[:, :], Act.Sign).then_inc(S.arst, 1)
+    SC.activation(T.rn[:, 0:16], T.on[:, 0:16], Act.Copy, scale=0.0).then_inc(S.arn, 1)
+    SC.activation(T.tmp[:, 0:128], T.on[:, 0:128], Act.Copy, scale=0.0).then_inc(S.atmp, 1)
+    SC.activation(T.tmp[:, 128:W], T.on[:, 0:W - 128], Act.Copy, scale=0.0).then_inc(S.atmp, 1)
 
     nv = [0]
 
@@ -151,89 +158,96 @@ def rank_program(g, core, T, topo):
     def vsync():
         V.wait_ge(S.vs, nv[0])
 
-    def slots(kt, dt_, rt, pt, st, ot, sem_r, sem_m):
-        vdone(V.tensor_scalar(dt_[:, :], kt[:, :], 4, None, Op.arith_shift_right))
-        vsync()
-        V.tensor_tensor(rt[:, :], dt_[:, 0:4].indirect(T.offc[:, 0:2]), T.pat[:, :], Op.is_equal).then_inc(sem_r, 1)
+    def slots(kt, dt_, rt, pt, st, ot, sem_d, sem_r, sem_m):
+        V.tensor_scalar(dt_[0:32, 1:5], kt[0:32, :], 4, None, Op.arith_shift_right).then_inc(sem_d, 1)
+        V.wait_ge(sem_d, 1)
+        V.tensor_tensor(rt[:, 16:48], dt_[:, 0:DW].indirect(T.offc[:, 0:2]), T.patd[:, :], Op.is_equal).then_inc(sem_r, 1)
         V.wait_ge(sem_m, 1)
         vdone(V.tensor_tensor_scan(st[:, :], T.rst[:, :], pt[:, 0:32], 0.0, Op.mult, Op.max))
         vsync()
         vdone(V.tensor_copy(ot[:, :], st[:, 7:32:8]))
 
-    V.memset(T.kw[64:128, :], 0).then_inc(S.kz, 1)
-    vdone(V.memset(T.packed[:, :], 0.0))
+    V.memset(T.on[:, :], 1.0).then_inc(S.cz, 1)
+    V.memset(T.dw[:, :], -1).then_inc(S.dz, 1)
     V.wait_ge(S.gu, 1)
     vdone(V.tensor_scalar(T.t1[:, :], T.ui[:, :], 3, 1, Op.arith_shift_right, Op.bitwise_and))
     vdone(V.tensor_scalar(T.t2[:, :], T.ui[:, :], 4, None, Op.arith_shift_right))
     vsync()
     vdone(V.tensor_tensor(T.t3[:, :], T.t1[:, :], T.t2[:, :], Op.add))
     vsync()
-    vdone(V.tensor_scalar(T.offc[:, :], T.t3[:, :], 0, 3, Op.max, Op.min))
+    vdone(V.tensor_copy(T.offc[:, :], T.t3[:, :]))
+    V.memset(T.kw[32:64, :], 0).then_inc(S.kz, 1)
+    V.memset(T.kw[64:128, :], 0).then_inc(S.kz, 1)
     V.wait_ge(S.gv, 1)
-    vdone(V.tensor_scalar(T.la[0:64, :], T.vv[0:64, :], 0.0, None, Op.is_ge))
-    vdone(V.tensor_scalar(T.lb[0:64, :], T.vv[0:64, :], 0.0, 255.0, Op.is_equal, Op.mult))
+    vdone(V.tensor_scalar(T.la[0:32, :], T.vv[0:32, :], 0.0, None, Op.is_ge))
+    vdone(V.tensor_scalar(T.lb[0:32, :], T.vv[0:32, :], 0.0, 255.0, Op.is_equal, Op.mult))
     vsync()
-    V.tensor_tensor(T.lh[0:64, :], T.la[0:64, :], T.lb[0:64, :], Op.add).then_inc(S.lhr, 1)
+    V.tensor_tensor(T.lh[0:32, :], T.la[0:32, :], T.lb[0:32, :], Op.add).then_inc(S.lhr, 1)
+    V.wait_ge(S.dz, 1)
     V.wait_ge(S.gd, 1)
-    vdone(V.tensor_scalar(T.rst[:, :], T.patd[:, :], 1.0, None, Op.min))
-    V.wait_ge(S.gp, 1)
-    V.wait_ge(S.kz, 1)
-    V.wait_ge(S.kl, 64)
-    vsync()
-    slots(T.kw, T.dw, T.rh, T.ps, T.seg, T.off, S.rhr, S.mm)
+    V.wait_ge(S.arst, 1)
+    V.wait_ge(S.kl, 32)
+    slots(T.kw, T.dw, T.rh, T.ps, T.seg, T.off, S.dwr, S.rhr, S.mm)
     V.wait_ge(S.xl, 16)
+    V.wait_ge(S.apk, 2)
     vsync()
     V.tensor_copy(T.packed[:, 0:W].indirect(T.off[:, 0:4]), T.xs[:, :]).then_inc(S.scat, 1)
     V.wait_ge(S.scat, 1)
-    me = slice(CAP * rank, CAP * rank + CAP)
-    V.tensor_copy(T.land[:, me], T.packed[:, me]).then_inc(S.own, 1)
-    vdone(V.memset(T.tmp[:, :], 0.0))
+    V.tensor_copy(T.land[:, blk(rank)], T.packed[:, blk(rank)]).then_inc(S["in%d" % rank], 1)
+    vdone(V.memset(T.dn[:, :], -1))
     V.wait_ge(S.kin, n_kin)
-    slots(T.kn, T.dn, T.rn, T.pn, T.sn, T.offn, S.rhn, S.mmn)
+    vsync()
+    slots(T.kn, T.dn, T.rn, T.pn, T.sn, T.offn, S.dnr, S.rhn, S.mmn)
     V.wait_ge(S.xin, n_xin)
+    V.wait_ge(S.atmp, 2)
     vsync()
     V.tensor_copy(T.tmp[:, 0:W].indirect(T.offn[:, 0:4]), T.xn[:, :]).then_inc(S.scatn, 1)
     V.wait_ge(S.scatn, 1)
-    V.tensor_copy(T.land[:, CAP * nrank:CAP * nrank + CAP], T.tmp[:, me]).then_inc(S.nbr, 1)
+    V.tensor_copy(T.land[:, blk(nrank)], T.tmp[:, blk(rank)]).then_inc(S["in%d" % nrank], 1)
 
-    PE.wait_ge(S.lhr, 1)
+    def count(pt, rt, sem_r, sem_m):
+        PE.matmul(pt[:, 0:32], T.on[0:1, :], T.crow[0:1, :], True, False)
+        PE.wait_ge(sem_r, 1)
+        PE.matmul(pt[:, 0:32], T.lh[0:32, :], rt[0:32, 16:48], False, False)
+        PE.matmul(pt[:, 0:32], T.on[0:32, :], rt[0:32, 0:32], False, True).then_inc(sem_m, 1)
+
+    PE.wait_ge(S.cz, 1)
+    PE.wait_ge(S.arh, 1)
     PE.wait_ge(S.gcst, 1)
-    PE.matmul(T.ps[:, 0:32], T.lh[0:1, :], T.crow[0:1, :], True, False)
-    PE.wait_ge(S.rhr, 1)
-    PE.matmul(T.ps[:, 0:32], T.lh[0:64, :], T.rh[0:64, :], False, True).then_inc(S.mm, 1)
-    PE.matmul(T.pn[:, 0:32], T.lh[0:1, :], T.crow[0:1, :], True, False)
-    PE.wait_ge(S.rhn, 1)
-    PE.matmul(T.pn[:, 0:32], T.lh[0:64, :], T.rn[0:64, :], False, True).then_inc(S.mmn, 1)
+    PE.wait_ge(S.lhr, 1)
+    count(T.ps, T.rh, S.rhr, S.mm)
+    PE.wait_ge(S.arn, 1)
+    count(T.pn, T.rn, S.rhn, S.mmn)
 
-    def fused(call):
+    def fused(trs_):
         trs = []
         cnt = 0
-        for kind, s, d, to, n, m in call:
-            rid, pid, _ = topo.addr(to)
+        for kind, s, d, to, engs, sem in trs_:
+            rid, pid, _ = topo.addr(cores[to])
             if kind == "dir":
-                src, dst, sem = T.packed[:, CAP * d:CAP * d + CAP], T.land[:, CAP * s:CAP * s + CAP], S.dirs
+                src, dst = T.packed[:, blk(d)], T.land[:, blk(s)]
             elif kind == "rly":
-                src, dst, sem = T.packed[:, CAP * d:CAP * d + CAP], T.rly[d], S.rin
+                src, dst = T.packed[:, blk(d)], T.rly[d]
             else:
-                src, dst, sem = T.rly[d], T.late[s], S["late%d" % s]
-            trs.append(RemoteDMATransfer(dst_ids=[DstId(rid=rid, pnc=pid)], dma_engine_mask=m, remote_sem=sem,
+                src, dst = T.rly[d], T.late[s]
+            trs.append(RemoteDMATransfer(dst_ids=[DstId(rid=rid, pnc=pid)], dma_engine_mask=_mask(engs), remote_sem=S[sem],
                                          src=src, dst=dst))
-            cnt += n
+            cnt += len(engs)
         g.remote_dma_fused(trs, local_sem=S.sent)
         return cnt
 
     nrid, npid, _ = topo.addr(nb)
-    g.wait_ge(S.kz, 1)
-    g.wait_ge(S.kl, 64)
-    g.remote_dma(T.kn[:, :], T.kw[:, :], S.kin, S.sent, npid, nrid, kmask[core])
-    n_sent = len(_bits(kmask[core]))
+    g.wait_ge(S.kz, 2)
+    g.wait_ge(S.kl, 32)
+    g.remote_dma(T.kn[:, :], T.kw[:, :], S.kin, S.sent, npid, nrid, kmask[rank])
+    g.wait_ge(S.xl, 16)
+    g.remote_dma(T.xn[:, :], T.xs[:, :], S.xin, S.sent, npid, nrid, xmask[rank])
+    n_sent = len(_bits(kmask[rank])) + len(_bits(xmask[rank]))
     g.wait_ge(S.scat, 1)
-    n_sent += fused(main[core])
-    g.remote_dma(T.xn[:, :], T.xs[:, :], S.xin, S.sent, npid, nrid, xmask[core])
-    n_sent += len(_bits(xmask[core]))
-    if core in hops:
-        g.wait_ge(S.rin, n_rin)
-        n_sent += fused(hops[core])
+    for w, trs in calls[rank]:
+        if w is not None:
+            g.wait_ge(S[w], arrive[w])
+        n_sent += fused(trs)
 
     runs = []
     for b in range(N):
@@ -243,16 +257,19 @@ def rank_program(g, core, T, topo):
             runs[-1][1] = b + 1
         else:
             runs.append([b, b + 1])
+    need = {}
+    for b in range(N):
+        if b not in late_in:
+            need[b] = 1 if (b == rank or b == nrank) else arrive["in%d" % b]
     n_st = 0
-    SC.wait_ge(S.dirs, n_dir)
-    SC.wait_ge(S.own, 1)
-    SC.wait_ge(S.nbr, 1)
-    for a, b in runs:
+    for a, b in sorted(runs, key=lambda r_: 0 if r_[0] <= rank < r_[1] and r_[1] - r_[0] <= 2 else 1):
+        for c in range(a, b):
+            SC.wait_ge(S["in%d" % c], need[c])
         SC.dma_start(T.y[:, CAP * a:CAP * b], T.land[:, CAP * a:CAP * b]).then_inc(S.stored, 16)
         n_st += 1
-    for s in sorted(late_in):
-        SY.wait_ge(S["late%d" % s], late_in[s])
-        SY.dma_start(T.y[:, CAP * s:CAP * s + CAP], T.late[s]).then_inc(S.stored, 16)
+    for s in late_in:
+        SY.wait_ge(S["late%d" % s], arrive["late%d" % s])
+        SY.dma_start(T.y[:, blk(s)], T.late[s]).then_inc(S.stored, 16)
         n_st += 1
 
     g.wait_ge(S.sent, n_sent)

@@ -5,7 +5,7 @@ from concourse.mybir import ActivationFunctionType as Act
 N = 6
 CAP = 32
 W = N * CAP
-DW = 12
+KW = 16
 
 SCRATCH = {
     "xs": ("sbuf", [128, 64], "float32"),
@@ -13,25 +13,21 @@ SCRATCH = {
     "packed": ("sbuf", [128, W], "float32"),
     "tmp": ("sbuf", [128, W], "float32"),
     "land": ("sbuf", [128, W], "float32"),
-    "kw": ("sbuf", [128, 4], "int32"),
-    "kn": ("sbuf", [128, 4], "int32"),
-    "dw": ("sbuf", [128, DW], "int32"),
-    "dn": ("sbuf", [128, DW], "int32"),
+    "kw": ("sbuf", [128, KW], "int32"),
+    "kn": ("sbuf", [128, KW], "int32"),
     "ui": ("sbuf", [128, 2], "int32"),
-    "t1": ("sbuf", [128, 2], "int32"),
-    "t2": ("sbuf", [128, 2], "int32"),
-    "t3": ("sbuf", [128, 2], "int32"),
     "offc": ("sbuf", [128, 2], "uint16"),
     "patd": ("sbuf", [128, 32], "float32"),
     "rst": ("sbuf", [128, 32], "float32"),
     "vv": ("sbuf", [128, 128], "bfloat16"),
-    "la": ("sbuf", [128, 128], "bfloat16"),
+    "ls": ("sbuf", [128, 128], "bfloat16"),
     "lb": ("sbuf", [128, 128], "bfloat16"),
-    "lh": ("sbuf", [128, 128], "bfloat16"),
+    "ln": ("sbuf", [128, 128], "bfloat16"),
     "on": ("sbuf", [128, 128], "bfloat16"),
+    "onn": ("sbuf", [128, 128], "bfloat16"),
     "crow": ("sbuf", [128, 32], "bfloat16"),
-    "rh": ("sbuf", [128, 48], "bfloat16"),
-    "rn": ("sbuf", [128, 48], "bfloat16"),
+    "rh": ("sbuf", [128, 56], "bfloat16"),
+    "rn": ("sbuf", [128, 56], "bfloat16"),
     "ps": ("psum", [128, 512], "float32"),
     "pn": ("psum", [128, 512], "float32"),
     "seg": ("sbuf", [128, 32], "float32"),
@@ -41,8 +37,9 @@ SCRATCH = {
     "rly": ("dram", [N, 128, CAP], "float32"),
     "late": ("dram", [N, 128, CAP], "float32"),
 }
-SEMAPHORES = (["kl", "xl", "kz", "dz", "dwr", "dnr", "gu", "gd", "gv", "gcst", "cz", "arh", "apk", "arst", "arn", "atmp",
-               "vs", "lhr", "rhr", "mm", "rhn", "mmn", "scat", "scatn", "kin", "xin", "sent", "stored", "rin0", "rin1"]
+SEMAPHORES = (["kl", "xl", "kz", "dz", "gu", "gd", "gv", "gcst", "cz", "arh", "apk", "arst", "arn", "atmp",
+               "vs", "ofr", "lhr", "rhr", "mm", "rhn", "mmn", "scat", "scatn", "kin", "xin", "sent", "stored", "rin0",
+               "rin1"]
               + ["late%d" % s for s in range(N)] + ["in%d" % s for s in range(N)])
 
 
@@ -130,22 +127,24 @@ def rank_program(g, core, T, topo):
     def blk(b):
         return slice(CAP * b, CAP * b + CAP)
 
-    SC.dma_start(T.kw[0:16, :], T.key[:, :]).then_inc(S.kl, 16)
-    SY.dma_start(T.kw[16:32, :], T.key[:, :]).then_inc(S.kl, 16)
+    SC.dma_start(T.kw[0:16, 4:8], T.key[:, :]).then_inc(S.kl, 16)
+    SY.dma_start(T.kw[16:32, 4:8], T.key[:, :]).then_inc(S.kl, 16)
     SY.dma_start(T.xs[:, :], T.x[:, :]).then_inc(S.xl, 16)
 
     g.iota(T.ui[:, :], [[32, 2]], 0, 1).then_inc(S.gu, 1)
     g.iota(T.vv[0:32, :], [[0, 8], [1, 16]], 16, -1, allow_small_or_imprecise_dtypes=True).then_inc(S.gv, 1)
-    g.iota(T.patd[:, :], [[0, 4], [1, 8]], 0, 0, allow_small_or_imprecise_dtypes=True).then_inc(S.gd, 1)
+    g.iota(T.patd[:, :], [[0, 4], [16, 8]], 0, 0, allow_small_or_imprecise_dtypes=True).then_inc(S.gd, 1)
 
-    SC.wait_ge(S.cz, 1)
+    SC.wait_ge(S.cz, 2)
     SC.activation(T.rh[:, 0:16], T.on[:, 0:16], Act.Copy, scale=0.0).then_inc(S.arh, 1)
+    SC.activation(T.rh[:, 48:56], T.on[:, 0:8], Act.Copy, scale=0.0).then_inc(S.arh, 1)
+    SC.wait_ge(S.gd, 1)
+    SC.activation(T.crow[0:1, :], T.patd[0:1, :], Act.Identity, bias=-256.0, scale=2.0).then_inc(S.gcst, 1)
+    SC.activation(T.rst[:, :], T.patd[:, :], Act.Sign).then_inc(S.arst, 1)
     SC.activation(T.packed[:, 0:128], T.on[:, 0:128], Act.Copy, scale=0.0).then_inc(S.apk, 1)
     SC.activation(T.packed[:, 128:W], T.on[:, 0:W - 128], Act.Copy, scale=0.0).then_inc(S.apk, 1)
-    SC.wait_ge(S.gd, 1)
-    SC.activation(T.crow[0:1, :], T.patd[0:1, :], Act.Identity, bias=-256.0, scale=32.0).then_inc(S.gcst, 1)
-    SC.activation(T.rst[:, :], T.patd[:, :], Act.Sign).then_inc(S.arst, 1)
     SC.activation(T.rn[:, 0:16], T.on[:, 0:16], Act.Copy, scale=0.0).then_inc(S.arn, 1)
+    SC.activation(T.rn[:, 48:56], T.on[:, 0:8], Act.Copy, scale=0.0).then_inc(S.arn, 1)
     SC.activation(T.tmp[:, 0:128], T.on[:, 0:128], Act.Copy, scale=0.0).then_inc(S.atmp, 1)
     SC.activation(T.tmp[:, 128:W], T.on[:, 0:W - 128], Act.Copy, scale=0.0).then_inc(S.atmp, 1)
 
@@ -158,46 +157,42 @@ def rank_program(g, core, T, topo):
     def vsync():
         V.wait_ge(S.vs, nv[0])
 
-    def slots(kt, dt_, rt, pt, st, ot, sem_d, sem_r, sem_m):
-        V.tensor_scalar(dt_[0:32, 1:5], kt[0:32, :], 4, None, Op.arith_shift_right).then_inc(sem_d, 1)
-        V.wait_ge(sem_d, 1)
-        V.tensor_tensor(rt[:, 16:48], dt_[:, 0:DW].indirect(T.offc[:, 0:2]), T.patd[:, :], Op.is_equal).then_inc(sem_r, 1)
+    def slots(kt, rt, pt, st, ot, sem_r, sem_m):
+        V.tensor_tensor(rt[:, 16:48], kt[:, 0:KW].indirect(T.offc[:, 0:2]), T.patd[:, :], Op.is_ge).then_inc(sem_r, 1)
+        V.wait_ge(S.arst, 1)
         V.wait_ge(sem_m, 1)
         vdone(V.tensor_tensor_scan(st[:, :], T.rst[:, :], pt[:, 0:32], 0.0, Op.mult, Op.max))
         vsync()
         vdone(V.tensor_copy(ot[:, :], st[:, 7:32:8]))
 
     V.memset(T.on[:, :], 1.0).then_inc(S.cz, 1)
-    V.memset(T.dw[:, :], -1).then_inc(S.dz, 1)
+    V.memset(T.onn[:, :], -1.0).then_inc(S.cz, 1)
+    V.memset(T.kw[32:64, 4:8], -1).then_inc(S.kz, 1)
+    V.memset(T.kw[64:128, 4:8], -1).then_inc(S.kz, 1)
+    V.memset(T.kw[:, 0:4], -1).then_inc(S.dz, 1)
+    V.memset(T.kw[:, 8:KW], -1).then_inc(S.dz, 1)
     V.wait_ge(S.gu, 1)
-    vdone(V.tensor_scalar(T.t1[:, :], T.ui[:, :], 3, 1, Op.arith_shift_right, Op.bitwise_and))
-    vdone(V.tensor_scalar(T.t2[:, :], T.ui[:, :], 4, None, Op.arith_shift_right))
-    vsync()
-    vdone(V.tensor_tensor(T.t3[:, :], T.t1[:, :], T.t2[:, :], Op.add))
-    vsync()
-    vdone(V.tensor_copy(T.offc[:, :], T.t3[:, :]))
-    V.memset(T.kw[32:64, :], 0).then_inc(S.kz, 1)
-    V.memset(T.kw[64:128, :], 0).then_inc(S.kz, 1)
+    V.tensor_scalar(T.offc[:, :], T.ui[:, :], 48.5, 0.0625, Op.add, Op.mult).then_inc(S.ofr, 1)
+    V.memset(T.kn[:, 0:4], -1).then_inc(S.dz, 1)
+    V.memset(T.kn[:, 8:KW], -1).then_inc(S.dz, 1)
     V.wait_ge(S.gv, 1)
-    vdone(V.tensor_scalar(T.la[0:32, :], T.vv[0:32, :], 0.0, None, Op.is_ge))
-    vdone(V.tensor_scalar(T.lb[0:32, :], T.vv[0:32, :], 0.0, 255.0, Op.is_equal, Op.mult))
-    vsync()
-    V.tensor_tensor(T.lh[0:32, :], T.la[0:32, :], T.lb[0:32, :], Op.add).then_inc(S.lhr, 1)
-    V.wait_ge(S.dz, 1)
+    V.tensor_scalar(T.ls[0:32, :], T.vv[0:32, :], 0.0, None, Op.is_gt).then_inc(S.lhr, 1)
+    V.tensor_scalar(T.lb[0:32, :], T.vv[0:32, :], 0.0, 256.0, Op.is_equal, Op.mult).then_inc(S.lhr, 1)
+    V.tensor_scalar(T.ln[0:32, :], T.vv[0:32, :], 0.0, -1.0, Op.is_gt, Op.mult).then_inc(S.lhr, 1)
+    V.wait_ge(S.kz, 2)
+    V.wait_ge(S.dz, 4)
+    V.wait_ge(S.ofr, 1)
     V.wait_ge(S.gd, 1)
-    V.wait_ge(S.arst, 1)
     V.wait_ge(S.kl, 32)
-    slots(T.kw, T.dw, T.rh, T.ps, T.seg, T.off, S.dwr, S.rhr, S.mm)
+    slots(T.kw, T.rh, T.ps, T.seg, T.off, S.rhr, S.mm)
     V.wait_ge(S.xl, 16)
     V.wait_ge(S.apk, 2)
     vsync()
     V.tensor_copy(T.packed[:, 0:W].indirect(T.off[:, 0:4]), T.xs[:, :]).then_inc(S.scat, 1)
     V.wait_ge(S.scat, 1)
     V.tensor_copy(T.land[:, blk(rank)], T.packed[:, blk(rank)]).then_inc(S["in%d" % rank], 1)
-    vdone(V.memset(T.dn[:, :], -1))
     V.wait_ge(S.kin, n_kin)
-    vsync()
-    slots(T.kn, T.dn, T.rn, T.pn, T.sn, T.offn, S.dnr, S.rhn, S.mmn)
+    slots(T.kn, T.rn, T.pn, T.sn, T.offn, S.rhn, S.mmn)
     V.wait_ge(S.xin, n_xin)
     V.wait_ge(S.atmp, 2)
     vsync()
@@ -208,15 +203,18 @@ def rank_program(g, core, T, topo):
     def count(pt, rt, sem_r, sem_m):
         PE.matmul(pt[:, 0:32], T.on[0:1, :], T.crow[0:1, :], True, False)
         PE.wait_ge(sem_r, 1)
-        PE.matmul(pt[:, 0:32], T.lh[0:32, :], rt[0:32, 16:48], False, False)
-        PE.matmul(pt[:, 0:32], T.on[0:32, :], rt[0:32, 0:32], False, True).then_inc(sem_m, 1)
+        PE.matmul(pt[:, 0:32], T.on[0:32, :], rt[0:32, 0:32], False, False)
+        PE.matmul(pt[:, 0:32], T.onn[0:32, :], rt[0:32, 1:33], False, False)
+        PE.matmul(pt[:, 0:32], T.ls[0:32, :], rt[0:32, 16:48], False, False)
+        PE.matmul(pt[:, 0:32], T.lb[0:32, :], rt[0:32, 16:48], False, False)
+        PE.matmul(pt[:, 0:32], T.ln[0:32, :], rt[0:32, 17:49], False, True).then_inc(sem_m, 1)
 
-    PE.wait_ge(S.cz, 1)
-    PE.wait_ge(S.arh, 1)
+    PE.wait_ge(S.cz, 2)
+    PE.wait_ge(S.arh, 2)
     PE.wait_ge(S.gcst, 1)
-    PE.wait_ge(S.lhr, 1)
+    PE.wait_ge(S.lhr, 3)
     count(T.ps, T.rh, S.rhr, S.mm)
-    PE.wait_ge(S.arn, 1)
+    PE.wait_ge(S.arn, 2)
     count(T.pn, T.rn, S.rhn, S.mmn)
 
     def fused(trs_):
@@ -239,7 +237,7 @@ def rank_program(g, core, T, topo):
     nrid, npid, _ = topo.addr(nb)
     g.wait_ge(S.kz, 2)
     g.wait_ge(S.kl, 32)
-    g.remote_dma(T.kn[:, :], T.kw[:, :], S.kin, S.sent, npid, nrid, kmask[rank])
+    g.remote_dma(T.kn[:, 4:8], T.kw[:, 4:8], S.kin, S.sent, npid, nrid, kmask[rank])
     g.wait_ge(S.xl, 16)
     g.remote_dma(T.xn[:, :], T.xs[:, :], S.xin, S.sent, npid, nrid, xmask[rank])
     n_sent = len(_bits(kmask[rank])) + len(_bits(xmask[rank]))
@@ -267,9 +265,10 @@ def rank_program(g, core, T, topo):
             SC.wait_ge(S["in%d" % c], need[c])
         SC.dma_start(T.y[:, CAP * a:CAP * b], T.land[:, CAP * a:CAP * b]).then_inc(S.stored, 16)
         n_st += 1
-    for s in late_in:
-        SY.wait_ge(S["late%d" % s], arrive["late%d" % s])
-        SY.dma_start(T.y[:, blk(s)], T.late[s]).then_inc(S.stored, 16)
+    for i, s in enumerate(late_in):
+        Q = SY if i % 2 == 0 else SC
+        Q.wait_ge(S["late%d" % s], arrive["late%d" % s])
+        Q.dma_start(T.y[:, blk(s)], T.late[s]).then_inc(S.stored, 16)
         n_st += 1
 
     g.wait_ge(S.sent, n_sent)

@@ -6,6 +6,7 @@ N = 6
 CAP = 32
 W = N * CAP
 KW = 16
+NSIM = 80
 
 SCRATCH = {
     "xs": ("sbuf", [128, 64], "float32"),
@@ -18,7 +19,7 @@ SCRATCH = {
     "ui": ("sbuf", [128, 2], "int32"),
     "offc": ("sbuf", [128, 2], "uint16"),
     "patd": ("sbuf", [128, 32], "float32"),
-    "rst": ("sbuf", [128, 32], "float32"),
+    "one": ("sbuf", [128, 8], "float32"),
     "vv": ("sbuf", [128, 128], "bfloat16"),
     "ls": ("sbuf", [128, 128], "bfloat16"),
     "lb": ("sbuf", [128, 128], "bfloat16"),
@@ -30,16 +31,14 @@ SCRATCH = {
     "rn": ("sbuf", [128, 56], "bfloat16"),
     "ps": ("psum", [128, 512], "float32"),
     "pn": ("psum", [128, 512], "float32"),
-    "seg": ("sbuf", [128, 32], "float32"),
-    "sn": ("sbuf", [128, 32], "float32"),
-    "off": ("sbuf", [128, 4], "uint16"),
-    "offn": ("sbuf", [128, 4], "uint16"),
+    "off": ("sbuf", [128, 32], "uint16"),
+    "offn": ("sbuf", [128, 32], "uint16"),
     "rly": ("dram", [N, 128, CAP], "float32"),
     "late": ("dram", [N, 128, CAP], "float32"),
 }
-SEMAPHORES = (["kl", "xl", "kz", "dz", "gu", "gd", "gv", "gcst", "cz", "arh", "apk", "arst", "arn", "atmp",
-               "vs", "ofr", "lhr", "rhr", "mm", "rhn", "mmn", "scat", "scatn", "kin", "xin", "sent", "stored", "rin0",
-               "rin1"]
+SEMAPHORES = (["kl", "xl", "kz", "dz", "dy", "gu", "gd", "gv", "gcst", "cz", "arh", "apk", "arn", "atmp",
+               "vs", "ofr", "lhr", "rhr", "mm", "rhn", "mmn", "scat", "scatn", "kin", "xin", "zin", "sent", "stored",
+               "rin0", "rin1"]
               + ["late%d" % s for s in range(N)] + ["in%d" % s for s in range(N)])
 
 
@@ -69,63 +68,102 @@ def _plan(cores, topo):
     def one_link(a, b):
         return 1 if (topo.mates(a, b) or topo.same_plane(a, b)) else 0
 
-    def reach(r, ch):
-        return all(topo.may_write(cores[r], cores[d]) for d in on_chip[ch])
+    def reach(c, ch):
+        return all(topo.may_write(c, cores[d]) for d in on_chip[ch])
 
     far = [sorted([ch for ch in on_chip if ch != chip[r]], key=lambda ch: (one_link(chip[r], ch), ch)) for r in range(n)]
-    passes = [[] for _ in range(n)]
+    calls, hmask = {}, {}
+    kmask, xmask, helper = [0] * n, [0] * n, [[] for _ in range(n)]
     for r in range(n):
-        for ch in far[r]:
-            if not reach(r, ch):
-                passes[nbr[r]].append((r, ch))
-
-    calls = [[] for _ in range(n)]
-    kmask, xmask = [0] * n, [0] * n
-    for r in range(n):
-        every = _bits(topo.mask(cores[r], cores[nbr[r]]))
-        out = [e for e in every if all((topo.mask(cores[r], cores[d]) >> e) & 1 for d in range(n) if chip[d] != chip[r])]
-        mine = [ch for ch in far[r] if reach(r, ch)]
-        relayed = [ch for ch in far[r] if not reach(r, ch)]
-        for ch in relayed:
-            parts = _split(every, len(on_chip[ch]))
-            sem = "rin%d" % passes[nbr[r]].index((r, ch))
-            calls[r].append((None, [("rly", r, d, nbr[r], parts[i], sem) for i, d in enumerate(on_chip[ch])]))
+        me = cores[r]
+        calls[me] = []
+        every = _bits(topo.mask(me, cores[nbr[r]]))
+        out = [e for e in every if all((topo.mask(me, cores[d]) >> e) & 1 for d in range(n) if chip[d] != chip[r])]
+        mine = [ch for ch in far[r] if reach(me, ch)]
+        relayed = [ch for ch in far[r] if not reach(me, ch)]
+        if relayed:
+            hs = [c for c in range(NSIM) if c not in cores and topo.chip(c) == chip[r] and topo.die(c) == topo.die(me)
+                  and all(reach(c, ch) for ch in relayed)][:max(len(on_chip[ch]) for ch in relayed)]
+            helper[r] = hs
+            for h in hs:
+                hmask[h] = _mask([e for e in _bits(topo.mask(h, me))
+                                  if all((topo.mask(h, cores[d]) >> e) & 1 for ch in relayed for d in on_chip[ch])])
+                calls[h] = []
+            for i, ch in enumerate(relayed):
+                parts = _split(every, len(on_chip[ch]))
+                calls[me].append((None, [("rly", r, d, hs[j % len(hs)], parts[j], "rin%d" % i)
+                                         for j, d in enumerate(on_chip[ch])]))
+                for k, h in enumerate(hs):
+                    ds = [d for j, d in enumerate(on_chip[ch]) if j % len(hs) == k]
+                    parts = _split(_bits(hmask[h]), len(ds))
+                    calls[h].append(("rin%d" % i, [("late", r, d, cores[d], parts[j], "late%d" % r)
+                                                   for j, d in enumerate(ds)]))
         db = [d for ch in mine for d in on_chip[ch]]
         if db:
             parts = _split(out, len(db))
-            calls[r].append((None, [("dir", r, d, d, parts[i], "in%d" % r) for i, d in enumerate(db)]))
+            calls[me].append((None, [("dir", r, d, cores[d], parts[i], "in%d" % r) for i, d in enumerate(db)]))
         used = every if relayed else out
         free = [e for e in every if e not in used]
         kmask[r], xmask[r] = _mask(used), _mask(free if free else used)
-        for i, (s, ch) in enumerate(passes[r]):
-            parts = _split(out, len(on_chip[ch]))
-            calls[r].append(("rin%d" % i, [("late", s, d, d, parts[j], "late%d" % s) for j, d in enumerate(on_chip[ch])]))
-    return calls, kmask, xmask, nbr
+    return calls, kmask, xmask, hmask, helper, nbr
 
 
 def rank_program(g, core, T, topo):
-    rank = T.rank_of(core)
-    if rank is None:
-        return
     cores = list(T.cores)
-    calls, kmask, xmask, nbrs = _plan(cores, topo)
-    nrank = nbrs[rank]
-    nb = cores[nrank]
+    calls, kmask, xmask, hmask, helper, nbrs = _plan(cores, topo)
+    if core not in calls:
+        return
+    rank = T.rank_of(core)
     S = T.sem
     V, PE, SY, SC = g.vector, g.tensor, g.sync, g.scalar
 
     arrive = {}
-    for r in range(N):
-        for _, trs in calls[r]:
+    for c_ in calls:
+        for _, trs in calls[c_]:
             for kind, s, d, to, engs, sem in trs:
-                if to == rank:
+                if to == core:
                     arrive[sem] = arrive.get(sem, 0) + len(engs)
-    late_in = [s for s in range(N) if "late%d" % s in arrive]
-    n_kin = len(_bits(kmask[nrank]))
-    n_xin = len(_bits(xmask[nrank]))
 
     def blk(b):
         return slice(CAP * b, CAP * b + CAP)
+
+    def fused(trs_):
+        trs = []
+        cnt = 0
+        for kind, s, d, to, engs, sem in trs_:
+            rid, pid, _ = topo.addr(to)
+            if kind == "dir":
+                src, dst = T.packed[:, blk(d)], T.land[:, blk(s)]
+            elif kind == "rly":
+                src, dst = T.packed[:, blk(d)], T.rly[d]
+            else:
+                src, dst = T.rly[d], T.late[s]
+            trs.append(RemoteDMATransfer(dst_ids=[DstId(rid=rid, pnc=pid)], dma_engine_mask=_mask(engs), remote_sem=S[sem],
+                                         src=src, dst=dst))
+            cnt += len(engs)
+        g.remote_dma_fused(trs, local_sem=S.sent)
+        return cnt
+
+    if rank is None:
+        r = [q for q in range(N) if core in helper[q]][0]
+        wd = CAP // len(helper[r])
+        a = CAP * r + wd * helper[r].index(core)
+        rid, pid, _ = topo.addr(cores[r])
+        V.memset(T.packed[:, 0:wd], 0.0).then_inc(S.cz, 1)
+        g.wait_ge(S.cz, 1)
+        g.remote_dma(T.tmp[:, a:a + wd], T.packed[:, 0:wd], S.zin, S.sent, pid, rid, hmask[core])
+        n_sent = len(_bits(hmask[core]))
+        for w, trs in calls[core]:
+            g.wait_ge(S[w], arrive[w])
+            n_sent += fused(trs)
+        g.wait_ge(S.sent, n_sent)
+        return
+
+    nrank = nbrs[rank]
+    nb = cores[nrank]
+    late_in = [s for s in range(N) if "late%d" % s in arrive]
+    n_kin = len(_bits(kmask[nrank]))
+    n_xin = len(_bits(xmask[nrank]))
 
     SC.dma_start(T.kw[0:16, 4:8], T.key[:, :]).then_inc(S.kl, 16)
     SY.dma_start(T.kw[16:32, 4:8], T.key[:, :]).then_inc(S.kl, 16)
@@ -140,13 +178,12 @@ def rank_program(g, core, T, topo):
     SC.activation(T.rh[:, 48:56], T.on[:, 0:8], Act.Copy, scale=0.0).then_inc(S.arh, 1)
     SC.wait_ge(S.gd, 1)
     SC.activation(T.crow[0:1, :], T.patd[0:1, :], Act.Identity, bias=-256.0, scale=2.0).then_inc(S.gcst, 1)
-    SC.activation(T.rst[:, :], T.patd[:, :], Act.Sign).then_inc(S.arst, 1)
     SC.activation(T.packed[:, 0:128], T.on[:, 0:128], Act.Copy, scale=0.0).then_inc(S.apk, 1)
     SC.activation(T.packed[:, 128:W], T.on[:, 0:W - 128], Act.Copy, scale=0.0).then_inc(S.apk, 1)
     SC.activation(T.rn[:, 0:16], T.on[:, 0:16], Act.Copy, scale=0.0).then_inc(S.arn, 1)
     SC.activation(T.rn[:, 48:56], T.on[:, 0:8], Act.Copy, scale=0.0).then_inc(S.arn, 1)
-    SC.activation(T.tmp[:, 0:128], T.on[:, 0:128], Act.Copy, scale=0.0).then_inc(S.atmp, 1)
-    SC.activation(T.tmp[:, 128:W], T.on[:, 0:W - 128], Act.Copy, scale=0.0).then_inc(S.atmp, 1)
+    if not helper[rank]:
+        SC.activation(T.tmp[:, blk(rank)], T.on[:, 0:CAP], Act.Copy, scale=0.0).then_inc(S.atmp, 1)
 
     nv = [0]
 
@@ -157,13 +194,13 @@ def rank_program(g, core, T, topo):
     def vsync():
         V.wait_ge(S.vs, nv[0])
 
-    def slots(kt, rt, pt, st, ot, sem_r, sem_m):
+    def compare(kt, rt, sem_r):
         V.tensor_tensor(rt[:, 16:48], kt[:, 0:KW].indirect(T.offc[:, 0:2]), T.patd[:, :], Op.is_ge).then_inc(sem_r, 1)
-        V.wait_ge(S.arst, 1)
+
+    def maxima(pt, ot, sem_m):
         V.wait_ge(sem_m, 1)
-        vdone(V.tensor_tensor_scan(st[:, :], T.rst[:, :], pt[:, 0:32], 0.0, Op.mult, Op.max))
-        vsync()
-        vdone(V.tensor_copy(ot[:, :], st[:, 7:32:8]))
+        for c in range(4):
+            vdone(V.tensor_tensor_scan(ot[:, c:32:4], T.one[:, :], pt[:, 8 * c:8 * c + 8], 0.0, Op.mult, Op.max))
 
     V.memset(T.on[:, :], 1.0).then_inc(S.cz, 1)
     V.memset(T.onn[:, :], -1.0).then_inc(S.cz, 1)
@@ -173,32 +210,35 @@ def rank_program(g, core, T, topo):
     V.memset(T.kw[:, 8:KW], -1).then_inc(S.dz, 1)
     V.wait_ge(S.gu, 1)
     V.tensor_scalar(T.offc[:, :], T.ui[:, :], 48.5, 0.0625, Op.add, Op.mult).then_inc(S.ofr, 1)
-    V.memset(T.kn[:, 0:4], -1).then_inc(S.dz, 1)
-    V.memset(T.kn[:, 8:KW], -1).then_inc(S.dz, 1)
     V.wait_ge(S.gv, 1)
     V.tensor_scalar(T.ls[0:32, :], T.vv[0:32, :], 0.0, None, Op.is_gt).then_inc(S.lhr, 1)
     V.tensor_scalar(T.lb[0:32, :], T.vv[0:32, :], 0.0, 256.0, Op.is_equal, Op.mult).then_inc(S.lhr, 1)
     V.tensor_scalar(T.ln[0:32, :], T.vv[0:32, :], 0.0, -1.0, Op.is_gt, Op.mult).then_inc(S.lhr, 1)
     V.wait_ge(S.kz, 2)
-    V.wait_ge(S.dz, 4)
+    V.wait_ge(S.dz, 2)
     V.wait_ge(S.ofr, 1)
     V.wait_ge(S.gd, 1)
     V.wait_ge(S.kl, 32)
-    slots(T.kw, T.rh, T.ps, T.seg, T.off, S.rhr, S.mm)
+    compare(T.kw, T.rh, S.rhr)
+    V.memset(T.one[:, :], 1.0).then_inc(S.dy, 1)
+    V.memset(T.kn[:, 0:4], -1).then_inc(S.dy, 1)
+    V.memset(T.kn[:, 8:KW], -1).then_inc(S.dy, 1)
+    V.wait_ge(S.dy, 3)
+    maxima(T.ps, T.off, S.mm)
     V.wait_ge(S.xl, 16)
     V.wait_ge(S.apk, 2)
     vsync()
-    V.tensor_copy(T.packed[:, 0:W].indirect(T.off[:, 0:4]), T.xs[:, :]).then_inc(S.scat, 1)
-    V.wait_ge(S.scat, 1)
-    V.tensor_copy(T.land[:, blk(rank)], T.packed[:, blk(rank)]).then_inc(S["in%d" % rank], 1)
+    V.tensor_copy(T.packed[:, 0:W].indirect(T.off[:, 28:32]), T.xs[:, :]).then_inc(S.scat, 1)
     V.wait_ge(S.kin, n_kin)
-    slots(T.kn, T.rn, T.pn, T.sn, T.offn, S.rhn, S.mmn)
+    compare(T.kn, T.rn, S.rhn)
+    maxima(T.pn, T.offn, S.mmn)
     V.wait_ge(S.xin, n_xin)
-    V.wait_ge(S.atmp, 2)
+    if not helper[rank]:
+        V.wait_ge(S.atmp, 1)
+    else:
+        V.wait_ge(S.zin, sum(len(_bits(hmask[h])) for h in helper[rank]))
     vsync()
-    V.tensor_copy(T.tmp[:, 0:W].indirect(T.offn[:, 0:4]), T.xn[:, :]).then_inc(S.scatn, 1)
-    V.wait_ge(S.scatn, 1)
-    V.tensor_copy(T.land[:, blk(nrank)], T.tmp[:, blk(rank)]).then_inc(S["in%d" % nrank], 1)
+    V.tensor_copy(T.tmp[:, 0:W].indirect(T.offn[:, 28:32]), T.xn[:, :]).then_inc(S.scatn, 1)
 
     def count(pt, rt, sem_r, sem_m):
         PE.matmul(pt[:, 0:32], T.on[0:1, :], T.crow[0:1, :], True, False)
@@ -217,59 +257,40 @@ def rank_program(g, core, T, topo):
     PE.wait_ge(S.arn, 2)
     count(T.pn, T.rn, S.rhn, S.mmn)
 
-    def fused(trs_):
-        trs = []
-        cnt = 0
-        for kind, s, d, to, engs, sem in trs_:
-            rid, pid, _ = topo.addr(cores[to])
-            if kind == "dir":
-                src, dst = T.packed[:, blk(d)], T.land[:, blk(s)]
-            elif kind == "rly":
-                src, dst = T.packed[:, blk(d)], T.rly[d]
-            else:
-                src, dst = T.rly[d], T.late[s]
-            trs.append(RemoteDMATransfer(dst_ids=[DstId(rid=rid, pnc=pid)], dma_engine_mask=_mask(engs), remote_sem=S[sem],
-                                         src=src, dst=dst))
-            cnt += len(engs)
-        g.remote_dma_fused(trs, local_sem=S.sent)
-        return cnt
-
     nrid, npid, _ = topo.addr(nb)
     g.wait_ge(S.kz, 2)
     g.wait_ge(S.kl, 32)
     g.remote_dma(T.kn[:, 4:8], T.kw[:, 4:8], S.kin, S.sent, npid, nrid, kmask[rank])
-    g.wait_ge(S.xl, 16)
-    g.remote_dma(T.xn[:, :], T.xs[:, :], S.xin, S.sent, npid, nrid, xmask[rank])
     n_sent = len(_bits(kmask[rank])) + len(_bits(xmask[rank]))
     g.wait_ge(S.scat, 1)
-    for w, trs in calls[rank]:
-        if w is not None:
-            g.wait_ge(S[w], arrive[w])
+    for w, trs in calls[core]:
         n_sent += fused(trs)
+    g.wait_ge(S.xl, 16)
+    g.remote_dma(T.xn[:, :], T.xs[:, :], S.xin, S.sent, npid, nrid, xmask[rank])
+
+    n_st = [0]
+
+    def store(Q, sems, out, in_):
+        for sem, cnt in sems:
+            Q.wait_ge(S[sem], cnt)
+        Q.dma_start(out, in_).then_inc(S.stored, 16)
+        n_st[0] += 1
 
     runs = []
     for b in range(N):
-        if b in late_in:
+        if b in late_in or b == rank or b == nrank:
             continue
         if runs and runs[-1][1] == b:
             runs[-1][1] = b + 1
         else:
             runs.append([b, b + 1])
-    need = {}
-    for b in range(N):
-        if b not in late_in:
-            need[b] = 1 if (b == rank or b == nrank) else arrive["in%d" % b]
-    n_st = 0
-    for a, b in sorted(runs, key=lambda r_: 0 if r_[0] <= rank < r_[1] and r_[1] - r_[0] <= 2 else 1):
-        for c in range(a, b):
-            SC.wait_ge(S["in%d" % c], need[c])
-        SC.dma_start(T.y[:, CAP * a:CAP * b], T.land[:, CAP * a:CAP * b]).then_inc(S.stored, 16)
-        n_st += 1
+    store(SC, [("scat", 1)], T.y[:, blk(rank)], T.packed[:, blk(rank)])
+    for a, b in runs:
+        store(SC, [("in%d" % c, arrive["in%d" % c]) for c in range(a, b)], T.y[:, CAP * a:CAP * b], T.land[:, CAP * a:CAP * b])
+    two = len(late_in) > 1
+    store(SY if two else SC, [("scatn", 1)], T.y[:, blk(nrank)], T.tmp[:, blk(rank)])
     for i, s in enumerate(late_in):
-        Q = SY if i % 2 == 0 else SC
-        Q.wait_ge(S["late%d" % s], arrive["late%d" % s])
-        Q.dma_start(T.y[:, blk(s)], T.late[s]).then_inc(S.stored, 16)
-        n_st += 1
+        store(SY if i % 2 == 0 else SC, [("late%d" % s, arrive["late%d" % s])], T.y[:, blk(s)], T.late[s])
 
     g.wait_ge(S.sent, n_sent)
-    g.wait_ge(S.stored, 16 * n_st)
+    g.wait_ge(S.stored, 16 * n_st[0])

from concourse.bass import DstId, RemoteDMATransfer
from concourse.mybir import AluOpType as Op
from concourse.mybir import ActivationFunctionType as Act

N = 6
CAP = 32
W = N * CAP
KW = 16
NSIM = 80

SCRATCH = {
    "xs": ("sbuf", [128, 64], "float32"),
    "xn": ("sbuf", [128, 64], "float32"),
    "packed": ("sbuf", [128, W], "float32"),
    "tmp": ("sbuf", [128, W], "float32"),
    "land": ("sbuf", [128, W], "float32"),
    "kw": ("sbuf", [128, KW], "int32"),
    "kn": ("sbuf", [128, KW], "int32"),
    "ui": ("sbuf", [128, 2], "int32"),
    "offc": ("sbuf", [128, 2], "uint16"),
    "patd": ("sbuf", [128, 32], "float32"),
    "one": ("sbuf", [128, 8], "float32"),
    "vv": ("sbuf", [128, 128], "bfloat16"),
    "ls": ("sbuf", [128, 128], "bfloat16"),
    "lb": ("sbuf", [128, 128], "bfloat16"),
    "ln": ("sbuf", [128, 128], "bfloat16"),
    "on": ("sbuf", [128, 128], "bfloat16"),
    "onn": ("sbuf", [128, 128], "bfloat16"),
    "crow": ("sbuf", [128, 32], "bfloat16"),
    "rh": ("sbuf", [128, 56], "bfloat16"),
    "rn": ("sbuf", [128, 56], "bfloat16"),
    "ps": ("psum", [128, 512], "float32"),
    "pn": ("psum", [128, 512], "float32"),
    "off": ("sbuf", [128, 32], "uint16"),
    "offn": ("sbuf", [128, 32], "uint16"),
    "rly": ("dram", [N, 128, CAP], "float32"),
    "late": ("dram", [N, 128, CAP], "float32"),
}
SEMAPHORES = (["kl", "xl", "kz", "dz", "dy", "gu", "gd", "gv", "gcst", "cz", "arh", "apk", "arn", "atmp",
               "vs", "ofr", "lhr", "rhr", "mm", "rhn", "mmn", "scat", "scatn", "kin", "xin", "zin", "sent", "stored",
               "rin0", "rin1"]
              + ["late%d" % s for s in range(N)] + ["in%d" % s for s in range(N)])


def _bits(m):
    return [e for e in range(m.bit_length()) if (m >> e) & 1]


def _mask(engs):
    return sum(1 << e for e in engs)


def _split(engs, k):
    n = 1
    while 2 * n * k <= len(engs):
        n *= 2
    return [engs[i * n:(i + 1) * n] for i in range(k)]


def _plan(cores, topo):
    n = len(cores)
    chip = [topo.chip(c) for c in cores]
    on_chip = {}
    for r in range(n):
        on_chip.setdefault(chip[r], []).append(r)
    nbr = [[q for q in on_chip[chip[r]] if q != r][0] for r in range(n)]

    def one_link(a, b):
        return 1 if (topo.mates(a, b) or topo.same_plane(a, b)) else 0

    def reach(c, ch):
        return all(topo.may_write(c, cores[d]) for d in on_chip[ch])

    far = [sorted([ch for ch in on_chip if ch != chip[r]], key=lambda ch: (one_link(chip[r], ch), ch)) for r in range(n)]
    calls, hmask = {}, {}
    kmask, xmask, helper = [0] * n, [0] * n, [[] for _ in range(n)]
    for r in range(n):
        me = cores[r]
        calls[me] = []
        every = _bits(topo.mask(me, cores[nbr[r]]))
        out = [e for e in every if all((topo.mask(me, cores[d]) >> e) & 1 for d in range(n) if chip[d] != chip[r])]
        mine = [ch for ch in far[r] if reach(me, ch)]
        relayed = [ch for ch in far[r] if not reach(me, ch)]
        if relayed:
            hs = [c for c in range(NSIM) if c not in cores and topo.chip(c) == chip[r] and topo.die(c) == topo.die(me)
                  and all(reach(c, ch) for ch in relayed)][:max(len(on_chip[ch]) for ch in relayed)]
            helper[r] = hs
            for h in hs:
                hmask[h] = _mask([e for e in _bits(topo.mask(h, me))
                                  if all((topo.mask(h, cores[d]) >> e) & 1 for ch in relayed for d in on_chip[ch])])
                calls[h] = []
            for i, ch in enumerate(relayed):
                parts = _split(every, len(on_chip[ch]))
                calls[me].append((None, [("rly", r, d, hs[j % len(hs)], parts[j], "rin%d" % i)
                                         for j, d in enumerate(on_chip[ch])]))
                for k, h in enumerate(hs):
                    ds = [d for j, d in enumerate(on_chip[ch]) if j % len(hs) == k]
                    parts = _split(_bits(hmask[h]), len(ds))
                    calls[h].append(("rin%d" % i, [("late", r, d, cores[d], parts[j], "late%d" % r)
                                                   for j, d in enumerate(ds)]))
        db = [d for ch in mine for d in on_chip[ch]]
        if db:
            parts = _split(out, len(db))
            calls[me].append((None, [("dir", r, d, cores[d], parts[i], "in%d" % r) for i, d in enumerate(db)]))
        used = every if relayed else out
        free = [e for e in every if e not in used]
        kmask[r], xmask[r] = _mask(used), _mask(free if free else used)
    return calls, kmask, xmask, hmask, helper, nbr


def rank_program(g, core, T, topo):
    cores = list(T.cores)
    calls, kmask, xmask, hmask, helper, nbrs = _plan(cores, topo)
    if core not in calls:
        return
    rank = T.rank_of(core)
    S = T.sem
    V, PE, SY, SC = g.vector, g.tensor, g.sync, g.scalar

    arrive = {}
    for c_ in calls:
        for _, trs in calls[c_]:
            for kind, s, d, to, engs, sem in trs:
                if to == core:
                    arrive[sem] = arrive.get(sem, 0) + len(engs)

    def blk(b):
        return slice(CAP * b, CAP * b + CAP)

    def fused(trs_):
        trs = []
        cnt = 0
        for kind, s, d, to, engs, sem in trs_:
            rid, pid, _ = topo.addr(to)
            if kind == "dir":
                src, dst = T.packed[:, blk(d)], T.land[:, blk(s)]
            elif kind == "rly":
                src, dst = T.packed[:, blk(d)], T.rly[d]
            else:
                src, dst = T.rly[d], T.late[s]
            trs.append(RemoteDMATransfer(dst_ids=[DstId(rid=rid, pnc=pid)], dma_engine_mask=_mask(engs), remote_sem=S[sem],
                                         src=src, dst=dst))
            cnt += len(engs)
        g.remote_dma_fused(trs, local_sem=S.sent)
        return cnt

    if rank is None:
        r = [q for q in range(N) if core in helper[q]][0]
        wd = CAP // len(helper[r])
        a = CAP * r + wd * helper[r].index(core)
        rid, pid, _ = topo.addr(cores[r])
        V.memset(T.packed[:, 0:wd], 0.0).then_inc(S.cz, 1)
        g.wait_ge(S.cz, 1)
        g.remote_dma(T.tmp[:, a:a + wd], T.packed[:, 0:wd], S.zin, S.sent, pid, rid, hmask[core])
        n_sent = len(_bits(hmask[core]))
        for w, trs in calls[core]:
            g.wait_ge(S[w], arrive[w])
            n_sent += fused(trs)
        g.wait_ge(S.sent, n_sent)
        return

    nrank = nbrs[rank]
    nb = cores[nrank]
    late_in = [s for s in range(N) if "late%d" % s in arrive]
    n_kin = len(_bits(kmask[nrank]))
    n_xin = len(_bits(xmask[nrank]))

    SC.dma_start(T.kw[0:16, 4:8], T.key[:, :]).then_inc(S.kl, 16)
    SY.dma_start(T.kw[16:32, 4:8], T.key[:, :]).then_inc(S.kl, 16)
    SY.dma_start(T.xs[:, :], T.x[:, :]).then_inc(S.xl, 16)

    g.iota(T.ui[:, :], [[32, 2]], 0, 1).then_inc(S.gu, 1)
    g.iota(T.vv[0:32, :], [[0, 8], [1, 16]], 16, -1, allow_small_or_imprecise_dtypes=True).then_inc(S.gv, 1)
    g.iota(T.patd[:, :], [[0, 4], [16, 8]], 0, 0, allow_small_or_imprecise_dtypes=True).then_inc(S.gd, 1)

    SC.wait_ge(S.cz, 2)
    SC.activation(T.rh[:, 0:16], T.on[:, 0:16], Act.Copy, scale=0.0).then_inc(S.arh, 1)
    SC.activation(T.rh[:, 48:56], T.on[:, 0:8], Act.Copy, scale=0.0).then_inc(S.arh, 1)
    SC.wait_ge(S.gd, 1)
    SC.activation(T.crow[0:1, :], T.patd[0:1, :], Act.Identity, bias=-256.0, scale=2.0).then_inc(S.gcst, 1)
    SC.activation(T.packed[:, 0:128], T.on[:, 0:128], Act.Copy, scale=0.0).then_inc(S.apk, 1)
    SC.activation(T.packed[:, 128:W], T.on[:, 0:W - 128], Act.Copy, scale=0.0).then_inc(S.apk, 1)
    SC.activation(T.rn[:, 0:16], T.on[:, 0:16], Act.Copy, scale=0.0).then_inc(S.arn, 1)
    SC.activation(T.rn[:, 48:56], T.on[:, 0:8], Act.Copy, scale=0.0).then_inc(S.arn, 1)
    if not helper[rank]:
        SC.activation(T.tmp[:, blk(rank)], T.on[:, 0:CAP], Act.Copy, scale=0.0).then_inc(S.atmp, 1)

    nv = [0]

    def vdone(ins):
        ins.then_inc(S.vs, 1)
        nv[0] += 1

    def vsync():
        V.wait_ge(S.vs, nv[0])

    def compare(kt, rt, sem_r):
        V.tensor_tensor(rt[:, 16:48], kt[:, 0:KW].indirect(T.offc[:, 0:2]), T.patd[:, :], Op.is_ge).then_inc(sem_r, 1)

    def maxima(pt, ot, sem_m):
        V.wait_ge(sem_m, 1)
        for c in range(4):
            vdone(V.tensor_tensor_scan(ot[:, c:32:4], T.one[:, :], pt[:, 8 * c:8 * c + 8], 0.0, Op.mult, Op.max))

    V.memset(T.on[:, :], 1.0).then_inc(S.cz, 1)
    V.memset(T.onn[:, :], -1.0).then_inc(S.cz, 1)
    V.memset(T.kw[32:64, 4:8], -1).then_inc(S.kz, 1)
    V.memset(T.kw[64:128, 4:8], -1).then_inc(S.kz, 1)
    V.memset(T.kw[:, 0:4], -1).then_inc(S.dz, 1)
    V.memset(T.kw[:, 8:KW], -1).then_inc(S.dz, 1)
    V.wait_ge(S.gu, 1)
    V.tensor_scalar(T.offc[:, :], T.ui[:, :], 48.5, 0.0625, Op.add, Op.mult).then_inc(S.ofr, 1)
    V.wait_ge(S.gv, 1)
    V.tensor_scalar(T.ls[0:32, :], T.vv[0:32, :], 0.0, None, Op.is_gt).then_inc(S.lhr, 1)
    V.tensor_scalar(T.lb[0:32, :], T.vv[0:32, :], 0.0, 256.0, Op.is_equal, Op.mult).then_inc(S.lhr, 1)
    V.tensor_scalar(T.ln[0:32, :], T.vv[0:32, :], 0.0, -1.0, Op.is_gt, Op.mult).then_inc(S.lhr, 1)
    V.wait_ge(S.kz, 2)
    V.wait_ge(S.dz, 2)
    V.wait_ge(S.ofr, 1)
    V.wait_ge(S.gd, 1)
    V.wait_ge(S.kl, 32)
    compare(T.kw, T.rh, S.rhr)
    V.memset(T.one[:, :], 1.0).then_inc(S.dy, 1)
    V.memset(T.kn[:, 0:4], -1).then_inc(S.dy, 1)
    V.memset(T.kn[:, 8:KW], -1).then_inc(S.dy, 1)
    V.wait_ge(S.dy, 3)
    maxima(T.ps, T.off, S.mm)
    V.wait_ge(S.xl, 16)
    V.wait_ge(S.apk, 2)
    vsync()
    V.tensor_copy(T.packed[:, 0:W].indirect(T.off[:, 28:32]), T.xs[:, :]).then_inc(S.scat, 1)
    V.wait_ge(S.kin, n_kin)
    compare(T.kn, T.rn, S.rhn)
    maxima(T.pn, T.offn, S.mmn)
    V.wait_ge(S.xin, n_xin)
    if not helper[rank]:
        V.wait_ge(S.atmp, 1)
    else:
        V.wait_ge(S.zin, sum(len(_bits(hmask[h])) for h in helper[rank]))
    vsync()
    V.tensor_copy(T.tmp[:, 0:W].indirect(T.offn[:, 28:32]), T.xn[:, :]).then_inc(S.scatn, 1)

    def count(pt, rt, sem_r, sem_m):
        PE.matmul(pt[:, 0:32], T.on[0:1, :], T.crow[0:1, :], True, False)
        PE.wait_ge(sem_r, 1)
        PE.matmul(pt[:, 0:32], T.on[0:32, :], rt[0:32, 0:32], False, False)
        PE.matmul(pt[:, 0:32], T.onn[0:32, :], rt[0:32, 1:33], False, False)
        PE.matmul(pt[:, 0:32], T.ls[0:32, :], rt[0:32, 16:48], False, False)
        PE.matmul(pt[:, 0:32], T.lb[0:32, :], rt[0:32, 16:48], False, False)
        PE.matmul(pt[:, 0:32], T.ln[0:32, :], rt[0:32, 17:49], False, True).then_inc(sem_m, 1)

    PE.wait_ge(S.cz, 2)
    PE.wait_ge(S.arh, 2)
    PE.wait_ge(S.gcst, 1)
    PE.wait_ge(S.lhr, 3)
    count(T.ps, T.rh, S.rhr, S.mm)
    PE.wait_ge(S.arn, 2)
    count(T.pn, T.rn, S.rhn, S.mmn)

    nrid, npid, _ = topo.addr(nb)
    g.wait_ge(S.kz, 2)
    g.wait_ge(S.kl, 32)
    g.remote_dma(T.kn[:, 4:8], T.kw[:, 4:8], S.kin, S.sent, npid, nrid, kmask[rank])
    n_sent = len(_bits(kmask[rank])) + len(_bits(xmask[rank]))
    g.wait_ge(S.scat, 1)
    for w, trs in calls[core]:
        n_sent += fused(trs)
    g.wait_ge(S.xl, 16)
    g.remote_dma(T.xn[:, :], T.xs[:, :], S.xin, S.sent, npid, nrid, xmask[rank])

    n_st = [0]

    def store(Q, sems, out, in_):
        for sem, cnt in sems:
            Q.wait_ge(S[sem], cnt)
        Q.dma_start(out, in_).then_inc(S.stored, 16)
        n_st[0] += 1

    runs = []
    for b in range(N):
        if b in late_in or b == rank or b == nrank:
            continue
        if runs and runs[-1][1] == b:
            runs[-1][1] = b + 1
        else:
            runs.append([b, b + 1])
    store(SC, [("scat", 1)], T.y[:, blk(rank)], T.packed[:, blk(rank)])
    for a, b in runs:
        store(SC, [("in%d" % c, arrive["in%d" % c]) for c in range(a, b)], T.y[:, CAP * a:CAP * b], T.land[:, CAP * a:CAP * b])
    two = len(late_in) > 1
    store(SY if two else SC, [("scatn", 1)], T.y[:, blk(nrank)], T.tmp[:, blk(rank)])
    for i, s in enumerate(late_in):
        store(SY if i % 2 == 0 else SC, [("late%d" % s, arrive["late%d" % s])], T.y[:, blk(s)], T.late[s])

    g.wait_ge(S.sent, n_sent)
    g.wait_ge(S.stored, 16 * n_st[0])
